import numpy as np
import ml_dtypes


def mxq(x, axis, fmt="e4m3"):
    dtype, down = {"e4m3": (ml_dtypes.float8_e4m3fn, 7), "e5m2": (ml_dtypes.float8_e5m2, 14)}[fmt]
    v = np.moveaxis(np.asarray(x, np.float32).astype(ml_dtypes.bfloat16).astype(np.float64), axis, -1)
    blocks = v.reshape(v.shape[:-1] + (-1, 32))
    amax = np.abs(blocks).max(-1, keepdims=True)
    byte = np.maximum(np.where(amax > 0, np.frexp(amax)[1] - 1 + 127, 0) - down, 1)
    scale = np.exp2(byte - 127.0)
    codes = (blocks / scale).astype(np.float32).astype(dtype).astype(np.float64)
    return np.moveaxis((codes * scale).reshape(v.shape), -1, axis)


WIDE = False


def mx_kscale(k):
    if not WIDE:
        return np.ones(k)
    levels = np.array([10, -10, 5, -5, 0])
    if k % 512:
        return np.exp2(np.random.permutation(np.resize(levels, k // 32))).repeat(32)
    a = np.empty((k // 512, 16))
    for p in range(k // 512):
        a[p, :8] = np.random.permutation(np.resize(levels, 8))
        for g in range(8):
            far = levels[np.abs(levels - a[p, g]) >= 10]
            a[p, g + 8] = far[np.random.randint(len(far))]
    return np.exp2(a.ravel()).repeat(32)


def f64(x):
    return np.asarray(x).astype(np.float64)


def striped(idx):
    return np.tile(idx.reshape(-1, 16).T, (8, 1)).astype(np.uint16)


def unstriped(offs):
    return offs[:16].T.reshape(-1).astype(np.int64)


def pack_weight(w):
    k, n = w.shape
    w = f64(np.asarray(w, np.float32).astype(ml_dtypes.bfloat16)).reshape(k // 32, 32, n)
    amax = np.abs(w).max(1)
    byte = np.clip(np.where(amax > 0, np.frexp(amax)[1] - 1 + 127 - 7, 1), 1, 254)
    scaled = (w * np.exp2(127.0 - byte)[:, None, :]).reshape(k, n).astype(np.float32)
    words = np.ascontiguousarray(scaled.reshape(k // 512, 128, 4, n).transpose(0, 1, 3, 2)).astype(ml_dtypes.float8_e4m3fn).view(np.uint8)
    return words, np.ascontiguousarray(byte.astype(np.uint8).reshape(k // 512, 16, n))


def unpack_weight(words, scales):
    g, p, n, _ = words.shape
    vals = np.ascontiguousarray(words).view(ml_dtypes.float8_e4m3fn).astype(np.float64) * np.repeat(np.exp2(scales.astype(np.float64) - 127.0), 8, axis=1)[..., None]
    return vals.transpose(0, 1, 3, 2).reshape(g * 512, n)


def planes(y):
    n, m = y.shape
    v = y.astype(np.float32).astype(ml_dtypes.bfloat16).astype(np.float64).reshape(n // 32, 32, m)
    top = np.abs(v).max(1)
    byte = np.clip(np.where(top > 0, np.frexp(top)[1] - 1 + 127 - 7, 1), 1, 254)
    codes = (v * np.exp2(127.0 - byte)[:, None, :]).reshape(n, m).astype(np.float32).astype(ml_dtypes.float8_e4m3fn).view(np.uint8)
    words = codes.reshape(n // 512, 128, 4, m).transpose(0, 1, 3, 2)
    return np.ascontiguousarray(words), np.ascontiguousarray(byte.astype(np.uint8).reshape(n // 512, 16, m))


def relu(v):
    return np.maximum(v, 0.0)


K, T, S, H, N = 1024, 4096, 1024, 512, 512
P = 2 ** 7


def setup_inputs():
    n = np.random.standard_normal
    s = mx_kscale(K)[:, None]
    u = mx_kscale(H)
    packed_xT = pack_weight(n((K, T)) * s)
    packed_w2 = pack_weight(n((H, N)) / np.sqrt(H) / u[:, None])
    return {
        "x_words": packed_xT[0],
        "x_scales": packed_xT[1],
        "w1": (n((K, H)) / np.sqrt(K) / s * u).astype(np.float32),
        "gain": (np.tile(np.random.uniform(0.5, 1.5, T), (P, 1))).astype(np.float32),
        "shift": (np.tile(0.5 * np.random.standard_normal(T), (P, 1))).astype(np.float32),
        "wsum": (n((H, 1)) * u[:, None]).astype(np.float32),
        "w2_words": packed_w2[0],
        "w2_scales": packed_w2[1],
        "offs": striped(np.random.permutation(T)[:S]),
    }


def reference(x_words, x_scales, w1, gain, shift, wsum, w2_words, w2_scales, offs):
    xq = unpack_weight(x_words, x_scales)[:, unstriped(offs)]
    y = mxq(f64(w1), 0, "e4m3").T @ xq
    g = f64(gain)[:1][:, unstriped(offs)]
    t = f64(shift)[:1][:, unstriped(offs)]
    h = relu(y * g + f64(wsum) * t)
    out_0 = unpack_weight(w2_words, w2_scales).T @ mxq(h, 0, "e4m3")
    return (out_0,) + planes(out_0)

@@ -1,0 +1,238 @@
+from contextlib import ExitStack
+
+import concourse.mybir as mybir
+from concourse.masks import make_identity
+
+K, T, S, H, N = 1024, 4096, 1024, 512, 512
+FLOPS = 2 * K * H * S + 2 * H * N * S
+BYTES = K * T + K * T // 32 + 4 * K * H + 8 * T + 4 * H + H * N + H * N // 32 + 128 * 64 * 2 + 4 * N * S + N * S + N * S // 32
+
+F32 = mybir.dt.float32
+BF16 = mybir.dt.bfloat16
+I32 = mybir.dt.int32
+U32 = mybir.dt.uint32
+U16 = mybir.dt.uint16
+U8 = mybir.dt.uint8
+FP8X4 = mybir.dt.float8_e4m3fn_x4
+MULT = mybir.AluOpType.mult
+ADD = mybir.AluOpType.add
+COPY = mybir.ActivationFunctionType.Copy
+RELU = mybir.ActivationFunctionType.Relu
+
+P = 128
+PASSES = K // 512
+TILES = S // P
+HALVES = 2
+HALF = H // HALVES
+
+
+def tile_picked_zdq_mlprelu_po_kernel(
+    tc, x_words, x_scales, w1, gain, shift, wsum, w2_words, w2_scales, offs, out_0, out_1, out_2
+):
+    nc = tc.nc
+    with ExitStack() as ctx:
+        keep = ctx.enter_context(tc.tile_pool(name="keep", bufs=1))
+        ring = ctx.enter_context(tc.tile_pool(name="ring", bufs=3))
+        rows_space = ctx.enter_context(tc.tile_pool(name="rows_space", bufs=1))
+        table_space = ctx.enter_context(tc.tile_pool(name="table_space", bufs=1))
+        scale_space = ctx.enter_context(tc.tile_pool(name="scale_space", bufs=1))
+        first_space = ctx.enter_context(tc.tile_pool(name="first_space", bufs=1))
+        psum = ctx.enter_context(tc.psum_pool(name="psum", bufs=2))
+
+        offsets = keep.tile([P, S // 16], U16, name="offsets")
+        nc.sync.dma_start(offsets[:], offs)
+        wsum_cols = table_space.tile([P, 4], F32, name="wsum_cols", offset=0)
+        nc.scalar.dma_start(wsum_cols[:], wsum.rearrange("(p t) o -> p (t o)", t=4))
+
+        x_table0 = first_space.tile([P, T], I32, name="x_table0", offset=0)
+        nc.sync.dma_start(x_table0[:], x_words[0].rearrange("p c b -> p (c b)").bitcast(I32))
+        w2_raw_scales = keep.tile([P, N], U8, name="w2_raw_scales")
+        nc.vector.memset(w2_raw_scales[:].bitcast(I32), 0)
+        for q in range(4):
+            nc.sync.dma_start(
+                w2_raw_scales[32 * q : 32 * q + 4, :].bitcast(I32), w2_scales[0, 4 * q : 4 * q + 4, :].bitcast(I32)
+            )
+
+        ident = keep.tile([P, P], F32, name="ident")
+        make_identity(nc, ident[:])
+
+        scale_table = scale_space.tile([P, T], U8, name="scale_table", offset=0)
+        nc.vector.memset(scale_table[:].bitcast(I32), 0)
+        for q in range(4):
+            nc.gpsimd.dma_start(
+                scale_table[32 * q : 32 * q + 8, :].bitcast(I32), x_scales[:, 4 * q : 4 * q + 4, :].bitcast(I32)
+            )
+
+        row_table = rows_space.tile([P, T], F32, name="row_table", offset=4064)
+        nc.vector.memset(row_table[:], 0.0)
+        nc.scalar.dma_start(row_table[0:1, :], gain[0:1, :])
+        nc.scalar.dma_start(row_table[64:65, :], shift[0:1, :])
+
+        wsum_rows = psum.tile([P, 4, P], F32, name="wsum_rows", tag="result")
+        for t in range(4):
+            nc.tensor.transpose(wsum_rows[:, t, :], wsum_cols[:, t : t + 1].to_broadcast([P, P]), ident[:])
+
+        x_table1 = table_space.tile([P, T], I32, name="x_table1", offset=0)
+        nc.sync.dma_start(x_table1[:], x_words[1].rearrange("p c b -> p (c b)").bitcast(I32))
+
+        picked_rows = keep.tile([P, S], F32, name="picked_rows")
+        nc.vector.tensor_copy(picked_rows[:], row_table[:].indirect(offsets[:]))
+
+        w1_raw = {}
+        for c in range(HALVES):
+            for o in range(PASSES):
+                raw = rows_space.tile([P, 4, HALF], F32, name="w1_raw%d%d" % (c, o), offset=6144 + 4096 * (2 * c + o))
+                rows = w1[512 * o : 512 * (o + 1), HALF * c : HALF * (c + 1)]
+                nc.sync.dma_start(raw[:], rows.rearrange("(p j) c -> p j c", j=4))
+                w1_raw[c, o] = raw
+        w2_raw = rows_space.tile([P, N], I32, name="w2_raw", offset=4096)
+        nc.sync.dma_start(w2_raw[:], w2_words[0].rearrange("p c b -> p (c b)").bitcast(I32))
+
+        x_code0 = rows_space.tile([P, S], U32, name="x_code0", align_bytes=64, offset=0)
+        nc.vector.tensor_copy(x_code0[:], x_table0[:].bitcast(U32).indirect(offsets[:]))
+        x_planes = first_space.tile([P, S], U8, name="x_planes", align_bytes=64, offset=0)
+        nc.vector.tensor_copy(x_planes[:], scale_table[:].indirect(offsets[:]))
+
+        w2_plane = keep.tile([P, N], U8, name="w2_plane", align_bytes=64)
+        nc.vector.tensor_copy(
+            w2_plane[:].rearrange("p (t m) -> p t m", t=4), w2_raw_scales[:].rearrange("p (m t) -> p t m", t=4)
+        )
+
+        x_code1 = scale_space.tile([P, S], U32, name="x_code1", align_bytes=64, offset=0)
+        nc.vector.tensor_copy(x_code1[:], x_table1[:].bitcast(U32).indirect(offsets[:]))
+        x_codes = [x_code0, x_code1]
+
+        factors = keep.tile([P, TILES, 2], F32, name="factors")
+        for b in range(2):
+            turned = psum.tile([P, 4, P], F32, name="turned", tag="turn")
+            for a in range(4):
+                jt = 4 * b + a
+                nc.tensor.transpose(turned[:, a, :], picked_rows[:, P * jt : P * (jt + 1)], ident[:])
+            nc.scalar.copy(factors[:, 4 * b : 4 * b + 4, :], turned[:, :, 0:P:64])
+
+        offsets_term = []
+        for jt in range(TILES):
+            term = keep.tile([P, H], F32, name="term%d" % jt)
+            nc.scalar.activation(
+                term[:].rearrange("p (u m e) -> p u m e", u=2, e=2),
+                wsum_rows[:].rearrange("p (u e) m -> p u m e", u=2),
+                COPY,
+                scale=factors[:, jt, 1:2],
+            )
+            offsets_term.append(term)
+
+        w1_codes, w1_plane = {}, {}
+        for c in range(HALVES):
+            grouped = []
+            for o in range(PASSES):
+                if o == 0:
+                    g = keep.tile([P, 4 * HALF], BF16, name="w1_grouped%d%d" % (c, o), align_bytes=64)
+                else:
+                    g = table_space.tile([P, 4 * HALF], BF16, name="w1_grouped%d%d" % (c, o), align_bytes=64, offset=2048 * c)
+                dst = g[:].rearrange("p (u m e j) -> p u m j e", u=2, e=2, j=4)
+                src = w1_raw[c, o][:].rearrange("p j (m u e) -> p u m j e", u=2, e=2)
+                if o == 0:
+                    nc.scalar.copy(dst, src)
+                else:
+                    nc.vector.tensor_copy(dst, src)
+                grouped.append(g)
+            for o in range(PASSES):
+                codes = table_space.tile([P, HALF], U32, name="w1_codes%d%d" % (c, o), align_bytes=64, offset=4096 + 1024 * (2 * c + o))
+                plane = keep.tile([P, HALF], U8, name="w1_plane%d%d" % (c, o), align_bytes=64)
+                nc.vector.quantize_mx(out=codes[:].bitcast(FP8X4), scales=plane[:], in_=grouped[o][:])
+                w1_codes[c, o], w1_plane[c, o] = codes, plane
+
+        w2_codes = keep.tile([P, N], I32, name="w2_codes", align_bytes=64)
+        nc.vector.tensor_copy(
+            w2_codes[:].rearrange("p (t m) -> p t m", t=4), w2_raw[:].rearrange("p (m t) -> p t m", t=4)
+        )
+
+        out_codes = keep.tile([P, S], U32, name="out_codes", align_bytes=64)
+        out_plane = keep.tile([P, S], U8, name="out_plane", align_bytes=64)
+        out_rows = out_0.rearrange("(p t) j -> p t j", t=4)
+        out_words = out_1[0].rearrange("p c b -> p (c b)").bitcast(I32)
+
+        pre = [keep.tile([P, H], BF16, name="pre%d" % jt) for jt in range(TILES)]
+        hidden, result, rounded = {}, {}, {}
+
+        def first_layer(jt, c):
+            cols = slice(P * jt, P * (jt + 1))
+            y = psum.tile([P, HALF], F32, name="y%d" % c, tag="y%d" % c)
+            for o in range(PASSES):
+                nc.tensor.matmul_mx(
+                    out=y[:],
+                    lhsT=x_codes[o][:, cols].bitcast(FP8X4),
+                    lhsT_scale=x_planes[4 * o : P, cols],
+                    rhs=w1_codes[c, o][:].bitcast(FP8X4),
+                    rhs_scale=w1_plane[c, o][:],
+                    start=(o == 0),
+                    stop=(o == PASSES - 1),
+                )
+            part = slice(P * c, P * (c + 1))
+            nc.vector.scalar_tensor_tensor(
+                out=pre[jt][:].rearrange("p (u r) -> p u r", u=2)[:, :, part],
+                in0=y[:].rearrange("p (u r) -> p u r", u=2),
+                scalar=factors[:, jt, 0:1],
+                in1=offsets_term[jt][:].rearrange("p (u r) -> p u r", u=2)[:, :, part],
+                op0=MULT,
+                op1=ADD,
+            )
+
+        def turn(jt):
+            turned = psum.tile([P, 2, P], F32, name="turned_pairs", tag="turn")
+            words = pre[jt][:].bitcast(F32)
+            for u in range(2):
+                nc.tensor.transpose(turned[:, u, :], words[:, P * u : P * (u + 1)], ident[:])
+            h = ring.tile([P, 4 * P], BF16, name="h", align_bytes=64)
+            nc.scalar.activation(
+                h[:].rearrange("p (j u e) -> p j u e", u=2, e=2),
+                turned[:].bitcast(BF16).rearrange("p u (j e) -> p j u e", e=2),
+                RELU,
+            )
+            hidden[jt] = h
+
+        def second_layer(jt):
+            codes = ring.tile([P, P], U32, name="h_codes", align_bytes=64)
+            plane = ring.tile([P, P], U8, name="h_plane", align_bytes=64)
+            nc.vector.quantize_mx(out=codes[:].bitcast(FP8X4), scales=plane[:], in_=hidden[jt][:])
+            acc = psum.tile([P, 4, P], F32, name="acc", tag="result")
+            for t in range(4):
+                nc.tensor.matmul_mx(
+                    out=acc[:, t, :],
+                    lhsT=w2_codes[:, P * t : P * (t + 1)].bitcast(FP8X4),
+                    lhsT_scale=w2_plane[:, P * t : P * (t + 1)],
+                    rhs=codes[:].bitcast(FP8X4),
+                    rhs_scale=plane[:],
+                    start=True,
+                    stop=True,
+                )
+            res = keep.tile([P, 4, P], F32, name="res%d" % jt)
+            nc.scalar.copy(res[:], acc[:])
+            nc.sync.dma_start(out_rows[:, :, P * jt : P * (jt + 1)], res[:])
+            result[jt] = res
+
+        def round_result(jt):
+            r = ring.tile([P, 4 * P], BF16, name="rounded", align_bytes=64)
+            nc.vector.tensor_copy(
+                r[:].rearrange("p (c i t) -> p c t i", i=4, t=4),
+                result[jt][:].rearrange("p t (c i) -> p c t i", i=4),
+            )
+            rounded[jt] = r
+
+        def quantise_result(jt):
+            cols = slice(P * jt, P * (jt + 1))
+            nc.vector.quantize_mx(out=out_codes[:, cols].bitcast(FP8X4), scales=out_plane[:, cols], in_=rounded[jt][:])
+            if jt % 2 == 1:
+                both = slice(P * (jt - 1), P * (jt + 1))
+                nc.sync.dma_start(out_words[:, both], out_codes[:, both].bitcast(I32))
+
+        stages = [lambda jt: (first_layer(jt, 0), first_layer(jt, 1)), turn, second_layer, round_result, quantise_result]
+        for step in range(TILES + len(stages) - 1):
+            for depth in reversed(range(len(stages))):
+                jt = step - depth
+                if 0 <= jt < TILES:
+                    stages[depth](jt)
+
+        for q in range(4):
+            queue = nc.sync if q % 2 == 0 else nc.scalar
+            queue.dma_start(out_2[0, 4 * q : 4 * q + 4, :].bitcast(I32), out_plane[32 * q : 32 * q + 4, :].bitcast(I32))

@@ -22,8 +22,7 @@ RELU = mybir.ActivationFunctionType.Relu
 P = 128
 PASSES = K // 512
 TILES = S // P
-HALVES = 2
-HALF = H // HALVES
+Y_BANKS = 3
 
 
 def tile_picked_zdq_mlprelu_po_kernel(
@@ -34,75 +33,109 @@ def tile_picked_zdq_mlprelu_po_kernel(
         keep = ctx.enter_context(tc.tile_pool(name="keep", bufs=1))
         ring = ctx.enter_context(tc.tile_pool(name="ring", bufs=3))
         rows_space = ctx.enter_context(tc.tile_pool(name="rows_space", bufs=1))
-        table_space = ctx.enter_context(tc.tile_pool(name="table_space", bufs=1))
-        scale_space = ctx.enter_context(tc.tile_pool(name="scale_space", bufs=1))
         first_space = ctx.enter_context(tc.tile_pool(name="first_space", bufs=1))
+        second_space = ctx.enter_context(tc.tile_pool(name="second_space", bufs=1))
+        scale_space = ctx.enter_context(tc.tile_pool(name="scale_space", bufs=1))
         psum = ctx.enter_context(tc.psum_pool(name="psum", bufs=2))
 
         offsets = keep.tile([P, S // 16], U16, name="offsets")
         nc.sync.dma_start(offsets[:], offs)
-        wsum_cols = table_space.tile([P, 4], F32, name="wsum_cols", offset=0)
+        wsum_cols = second_space.tile([P, 4], F32, name="wsum_cols", offset=0)
         nc.scalar.dma_start(wsum_cols[:], wsum.rearrange("(p t) o -> p (t o)", t=4))
 
+        def w1_rows(o):
+            return w1[512 * o : 512 * (o + 1), :].rearrange("(p j) c -> p j c", j=4)
+
+        w1_raw0 = keep.tile([P, 4, H], F32, name="w1_raw0")
+        nc.sync.dma_start(w1_raw0[:], w1_rows(0))
+        w2_raw = keep.tile([P, N], I32, name="w2_raw")
+        nc.sync.dma_start(w2_raw[:], w2_words[0].rearrange("p c b -> p (c b)").bitcast(I32))
+
+        zeros = first_space.tile([P, P], F32, name="zeros", offset=4 * T - 256)
+        nc.vector.memset(zeros[:], 0.0)
+        scale_table = scale_space.tile([P, T], U8, name="scale_table", offset=0)
+        nc.vector.memset(scale_table[:].bitcast(I32), 0)
+        nc.scalar.dma_start(scale_table[0:P:4, :].bitcast(I32), x_scales.rearrange("o q c -> (o q) c").bitcast(I32))
+
+        row_table = rows_space.tile([P, T], F32, name="row_table", offset=0)
+        nc.vector.tensor_copy(
+            row_table[:].rearrange("p (a b) -> p a b", b=P), zeros[:].unsqueeze(1).to_broadcast([P, T // P, P])
+        )
+        nc.sync.dma_start(row_table[0:1, :], gain[0:1, :])
+        nc.sync.dma_start(row_table[64:65, :], shift[0:1, :])
+
+        ident = keep.tile([P, P], F32, name="ident")
+        nc.vector.tensor_copy(ident[:], zeros[:])
+        make_identity(nc, ident[:], nomemset=True)
+
+        w1_raw1 = first_space.tile([P, 4, H], F32, name="w1_raw1", offset=4 * T)
+        nc.sync.dma_start(w1_raw1[:], w1_rows(1))
         x_table0 = first_space.tile([P, T], I32, name="x_table0", offset=0)
         nc.sync.dma_start(x_table0[:], x_words[0].rearrange("p c b -> p (c b)").bitcast(I32))
+
+        x_planes = [keep.tile([P, S], U8, name="x_plane%d" % o, align_bytes=64) for o in range(PASSES)]
+        for plane in x_planes:
+            nc.vector.memset(plane[:].bitcast(I32), 0)
         w2_raw_scales = keep.tile([P, N], U8, name="w2_raw_scales")
         nc.vector.memset(w2_raw_scales[:].bitcast(I32), 0)
         for q in range(4):
-            nc.sync.dma_start(
+            nc.gpsimd.dma_start(
                 w2_raw_scales[32 * q : 32 * q + 4, :].bitcast(I32), w2_scales[0, 4 * q : 4 * q + 4, :].bitcast(I32)
             )
 
-        ident = keep.tile([P, P], F32, name="ident")
-        make_identity(nc, ident[:])
-
-        scale_table = scale_space.tile([P, T], U8, name="scale_table", offset=0)
-        nc.vector.memset(scale_table[:].bitcast(I32), 0)
-        for q in range(4):
-            nc.gpsimd.dma_start(
-                scale_table[32 * q : 32 * q + 8, :].bitcast(I32), x_scales[:, 4 * q : 4 * q + 4, :].bitcast(I32)
-            )
-
-        row_table = rows_space.tile([P, T], F32, name="row_table", offset=4064)
-        nc.vector.memset(row_table[:], 0.0)
-        nc.scalar.dma_start(row_table[0:1, :], gain[0:1, :])
-        nc.scalar.dma_start(row_table[64:65, :], shift[0:1, :])
-
-        wsum_rows = psum.tile([P, 4, P], F32, name="wsum_rows", tag="result")
+        wsum_rows = psum.tile([P, 4, P], F32, name="wsum_rows", tag="result", bufs=3)
         for t in range(4):
             nc.tensor.transpose(wsum_rows[:, t, :], wsum_cols[:, t : t + 1].to_broadcast([P, P]), ident[:])
 
-        x_table1 = table_space.tile([P, T], I32, name="x_table1", offset=0)
+        x_table1 = second_space.tile([P, T], I32, name="x_table1", offset=0)
         nc.sync.dma_start(x_table1[:], x_words[1].rearrange("p c b -> p (c b)").bitcast(I32))
 
         picked_rows = keep.tile([P, S], F32, name="picked_rows")
         nc.vector.tensor_copy(picked_rows[:], row_table[:].indirect(offsets[:]))
+        picked_scales = rows_space.tile([P, S], U8, name="picked_scales", offset=4 * S)
+        nc.vector.tensor_copy(picked_scales[:], scale_table[:].indirect(offsets[:]))
 
-        w1_raw = {}
-        for c in range(HALVES):
-            for o in range(PASSES):
-                raw = rows_space.tile([P, 4, HALF], F32, name="w1_raw%d%d" % (c, o), offset=6144 + 4096 * (2 * c + o))
-                rows = w1[512 * o : 512 * (o + 1), HALF * c : HALF * (c + 1)]
-                nc.sync.dma_start(raw[:], rows.rearrange("(p j) c -> p j c", j=4))
-                w1_raw[c, o] = raw
-        w2_raw = rows_space.tile([P, N], I32, name="w2_raw", offset=4096)
-        nc.sync.dma_start(w2_raw[:], w2_words[0].rearrange("p c b -> p (c b)").bitcast(I32))
+        queues = [[nc.scalar] * 4, [nc.sync] * 3 + [nc.gpsimd]]
+        for o in range(PASSES):
+            for q in range(4):
+                first = 4 * (16 * o + 4 * q)
+                queues[o][q].dma_start(
+                    x_planes[o][32 * q : 32 * q + 4, :].bitcast(I32),
+                    picked_scales[first : first + 16 : 4, :].bitcast(I32),
+                )
 
-        x_code0 = rows_space.tile([P, S], U32, name="x_code0", align_bytes=64, offset=0)
+        x_code0 = scale_space.tile([P, S], U32, name="x_code0", align_bytes=64, offset=0)
         nc.vector.tensor_copy(x_code0[:], x_table0[:].bitcast(U32).indirect(offsets[:]))
-        x_planes = first_space.tile([P, S], U8, name="x_planes", align_bytes=64, offset=0)
-        nc.vector.tensor_copy(x_planes[:], scale_table[:].indirect(offsets[:]))
 
-        w2_plane = keep.tile([P, N], U8, name="w2_plane", align_bytes=64)
+        w2_codes = keep.tile([P, N], I32, name="w2_codes", align_bytes=64)
+        nc.vector.tensor_copy(
+            w2_codes[:].rearrange("p (t m) -> p t m", t=4), w2_raw[:].rearrange("p (m t) -> p t m", t=4)
+        )
+        w2_plane = first_space.tile([P, N], U8, name="w2_plane", align_bytes=64, offset=0)
         nc.vector.tensor_copy(
             w2_plane[:].rearrange("p (t m) -> p t m", t=4), w2_raw_scales[:].rearrange("p (m t) -> p t m", t=4)
         )
 
-        x_code1 = scale_space.tile([P, S], U32, name="x_code1", align_bytes=64, offset=0)
-        nc.vector.tensor_copy(x_code1[:], x_table1[:].bitcast(U32).indirect(offsets[:]))
-        x_codes = [x_code0, x_code1]
+        x_code1 = [keep.tile([P, S // 2], U32, name="x_code1%d" % half, align_bytes=64) for half in range(2)]
+        for half in range(2):
+            nc.vector.tensor_copy(
+                x_code1[half][:], x_table1[:].bitcast(U32).indirect(offsets[:, S // 32 * half : S // 32 * (half + 1)])
+            )
 
-        factors = keep.tile([P, TILES, 2], F32, name="factors")
+        w1_codes, w1_plane = [], []
+        for o, raw in enumerate([w1_raw0, w1_raw1]):
+            g = keep.tile([P, 4 * H], BF16, name="w1_grouped%d" % o, align_bytes=64)
+            nc.scalar.copy(
+                g[:].rearrange("p (u m e j) -> p u m j e", u=2, e=2, j=4),
+                raw[:].rearrange("p j (m u e) -> p u m j e", u=2, e=2),
+            )
+            codes = keep.tile([P, H], U32, name="w1_codes%d" % o, align_bytes=64)
+            plane = keep.tile([P, H], U8, name="w1_plane%d" % o, align_bytes=64)
+            nc.vector.quantize_mx(out=codes[:].bitcast(FP8X4), scales=plane[:], in_=g[:])
+            w1_codes.append(codes)
+            w1_plane.append(plane)
+
+        factors = first_space.tile([P, TILES, 2], F32, name="factors", offset=4 * T + 256)
         for b in range(2):
             turned = psum.tile([P, 4, P], F32, name="turned", tag="turn")
             for a in range(4):
@@ -121,117 +154,125 @@ def tile_picked_zdq_mlprelu_po_kernel(
             )
             offsets_term.append(term)
 
-        w1_codes, w1_plane = {}, {}
-        for c in range(HALVES):
-            grouped = []
-            for o in range(PASSES):
-                if o == 0:
-                    g = keep.tile([P, 4 * HALF], BF16, name="w1_grouped%d%d" % (c, o), align_bytes=64)
-                else:
-                    g = table_space.tile([P, 4 * HALF], BF16, name="w1_grouped%d%d" % (c, o), align_bytes=64, offset=2048 * c)
-                dst = g[:].rearrange("p (u m e j) -> p u m j e", u=2, e=2, j=4)
-                src = w1_raw[c, o][:].rearrange("p j (m u e) -> p u m j e", u=2, e=2)
-                if o == 0:
-                    nc.scalar.copy(dst, src)
-                else:
-                    nc.vector.tensor_copy(dst, src)
-                grouped.append(g)
-            for o in range(PASSES):
-                codes = table_space.tile([P, HALF], U32, name="w1_codes%d%d" % (c, o), align_bytes=64, offset=4096 + 1024 * (2 * c + o))
-                plane = keep.tile([P, HALF], U8, name="w1_plane%d%d" % (c, o), align_bytes=64)
-                nc.vector.quantize_mx(out=codes[:].bitcast(FP8X4), scales=plane[:], in_=grouped[o][:])
-                w1_codes[c, o], w1_plane[c, o] = codes, plane
-
-        w2_codes = keep.tile([P, N], I32, name="w2_codes", align_bytes=64)
-        nc.vector.tensor_copy(
-            w2_codes[:].rearrange("p (t m) -> p t m", t=4), w2_raw[:].rearrange("p (m t) -> p t m", t=4)
-        )
-
-        out_codes = keep.tile([P, S], U32, name="out_codes", align_bytes=64)
         out_plane = keep.tile([P, S], U8, name="out_plane", align_bytes=64)
         out_rows = out_0.rearrange("(p t) j -> p t j", t=4)
         out_words = out_1[0].rearrange("p c b -> p (c b)").bitcast(I32)
 
         pre = [keep.tile([P, H], BF16, name="pre%d" % jt) for jt in range(TILES)]
-        hidden, result, rounded = {}, {}, {}
+        hidden, hidden_mx, result, rounded = {}, {}, {}, {}
 
-        def first_layer(jt, c):
+        sums = {}
+
+        def first_pass(jt):
             cols = slice(P * jt, P * (jt + 1))
-            y = psum.tile([P, HALF], F32, name="y%d" % c, tag="y%d" % c)
-            for o in range(PASSES):
-                nc.tensor.matmul_mx(
-                    out=y[:],
-                    lhsT=x_codes[o][:, cols].bitcast(FP8X4),
-                    lhsT_scale=x_planes[4 * o : P, cols],
-                    rhs=w1_codes[c, o][:].bitcast(FP8X4),
-                    rhs_scale=w1_plane[c, o][:],
-                    start=(o == 0),
-                    stop=(o == PASSES - 1),
-                )
-            part = slice(P * c, P * (c + 1))
-            nc.vector.scalar_tensor_tensor(
-                out=pre[jt][:].rearrange("p (u r) -> p u r", u=2)[:, :, part],
-                in0=y[:].rearrange("p (u r) -> p u r", u=2),
-                scalar=factors[:, jt, 0:1],
-                in1=offsets_term[jt][:].rearrange("p (u r) -> p u r", u=2)[:, :, part],
-                op0=MULT,
-                op1=ADD,
+            y = psum.tile([P, H], F32, name="y", bufs=Y_BANKS)
+            nc.tensor.matmul_mx(
+                out=y[:],
+                lhsT=x_code0[:, cols].bitcast(FP8X4),
+                lhsT_scale=x_planes[0][:, cols],
+                rhs=w1_codes[0][:].bitcast(FP8X4),
+                rhs_scale=w1_plane[0][:],
+                start=True,
+                stop=False,
             )
+            sums[jt] = y
 
-        def turn(jt):
-            turned = psum.tile([P, 2, P], F32, name="turned_pairs", tag="turn")
-            words = pre[jt][:].bitcast(F32)
-            for u in range(2):
-                nc.tensor.transpose(turned[:, u, :], words[:, P * u : P * (u + 1)], ident[:])
-            h = ring.tile([P, 4 * P], BF16, name="h", align_bytes=64)
+        def first_layer(first, count):
+            for jt in range(first, first + count):
+                if jt not in sums:
+                    first_pass(jt)
+                half, place = divmod(jt, TILES // 2)
+                nc.tensor.matmul_mx(
+                    out=sums[jt][:],
+                    lhsT=x_code1[half][:, P * place : P * (place + 1)].bitcast(FP8X4),
+                    lhsT_scale=x_planes[1][:, P * jt : P * (jt + 1)],
+                    rhs=w1_codes[1][:].bitcast(FP8X4),
+                    rhs_scale=w1_plane[1][:],
+                    start=False,
+                    stop=True,
+                )
+                nc.vector.scalar_tensor_tensor(
+                    out=pre[jt][:],
+                    in0=sums[jt][:],
+                    scalar=factors[:, jt, 0:1],
+                    in1=offsets_term[jt][:],
+                    op0=MULT,
+                    op1=ADD,
+                )
+
+        def turn(first, count):
+            n = P * count
+            turned = psum.tile([P, 2, n], F32, name="turned_pairs", tag="turn")
+            for a in range(count):
+                words = pre[first + a][:].bitcast(F32)
+                for u in range(2):
+                    nc.tensor.transpose(turned[:, u, P * a : P * (a + 1)], words[:, P * u : P * (u + 1)], ident[:])
+            h = ring.tile([P, 4 * n], BF16, name="h", align_bytes=64)
             nc.scalar.activation(
                 h[:].rearrange("p (j u e) -> p j u e", u=2, e=2),
                 turned[:].bitcast(BF16).rearrange("p u (j e) -> p j u e", e=2),
                 RELU,
             )
-            hidden[jt] = h
+            hidden[first] = h
 
-        def second_layer(jt):
-            codes = ring.tile([P, P], U32, name="h_codes", align_bytes=64)
-            plane = ring.tile([P, P], U8, name="h_plane", align_bytes=64)
-            nc.vector.quantize_mx(out=codes[:].bitcast(FP8X4), scales=plane[:], in_=hidden[jt][:])
-            acc = psum.tile([P, 4, P], F32, name="acc", tag="result")
-            for t in range(4):
-                nc.tensor.matmul_mx(
-                    out=acc[:, t, :],
-                    lhsT=w2_codes[:, P * t : P * (t + 1)].bitcast(FP8X4),
-                    lhsT_scale=w2_plane[:, P * t : P * (t + 1)],
-                    rhs=codes[:].bitcast(FP8X4),
-                    rhs_scale=plane[:],
-                    start=True,
-                    stop=True,
-                )
-            res = keep.tile([P, 4, P], F32, name="res%d" % jt)
-            nc.scalar.copy(res[:], acc[:])
-            nc.sync.dma_start(out_rows[:, :, P * jt : P * (jt + 1)], res[:])
-            result[jt] = res
+        def quantise_hidden(first, count):
+            n = P * count
+            codes = ring.tile([P, n], U32, name="h_codes", align_bytes=64)
+            plane = ring.tile([P, n], U8, name="h_plane", align_bytes=64)
+            nc.vector.quantize_mx(out=codes[:].bitcast(FP8X4), scales=plane[:], in_=hidden[first][:])
+            hidden_mx[first] = (codes, plane)
 
-        def round_result(jt):
-            r = ring.tile([P, 4 * P], BF16, name="rounded", align_bytes=64)
+        def second_layer(first, count):
+            n = P * count
+            codes, plane = hidden_mx[first]
+            res = keep.tile([P, 4, n], F32, name="res%d" % first)
+            per_bank = 4 // count
+            for bank in range(count):
+                acc = psum.tile([P, per_bank, n], F32, name="acc", tag="result", bufs=3)
+                for s in range(per_bank):
+                    t = per_bank * bank + s
+                    nc.tensor.matmul_mx(
+                        out=acc[:, s, :],
+                        lhsT=w2_codes[:, P * t : P * (t + 1)].bitcast(FP8X4),
+                        lhsT_scale=w2_plane[:, P * t : P * (t + 1)],
+                        rhs=codes[:].bitcast(FP8X4),
+                        rhs_scale=plane[:],
+                        start=True,
+                        stop=True,
+                    )
+                nc.scalar.copy(res[:, per_bank * bank : per_bank * (bank + 1), :], acc[:])
+            nc.sync.dma_start(out_rows[:, :, P * first : P * first + n], res[:])
+            result[first] = res
+
+        def round_result(first, count):
+            r = ring.tile([P, 4 * P * count], BF16, name="rounded", align_bytes=64)
             nc.vector.tensor_copy(
                 r[:].rearrange("p (c i t) -> p c t i", i=4, t=4),
-                result[jt][:].rearrange("p t (c i) -> p c t i", i=4),
+                result[first][:].rearrange("p t (c i) -> p c t i", i=4),
             )
-            rounded[jt] = r
+            rounded[first] = r
 
-        def quantise_result(jt):
-            cols = slice(P * jt, P * (jt + 1))
-            nc.vector.quantize_mx(out=out_codes[:, cols].bitcast(FP8X4), scales=out_plane[:, cols], in_=rounded[jt][:])
-            if jt % 2 == 1:
-                both = slice(P * (jt - 1), P * (jt + 1))
-                nc.sync.dma_start(out_words[:, both], out_codes[:, both].bitcast(I32))
+        def quantise_result(first, count):
+            cols = slice(P * first, P * (first + count))
+            codes = keep.tile([P, P * count], U32, name="out_codes%d" % first, align_bytes=64)
+            nc.vector.quantize_mx(out=codes[:].bitcast(FP8X4), scales=out_plane[:, cols], in_=rounded[first][:])
+            nc.sync.dma_start(out_words[:, cols], codes[:].bitcast(I32))
 
-        stages = [lambda jt: (first_layer(jt, 0), first_layer(jt, 1)), turn, second_layer, round_result, quantise_result]
-        for step in range(TILES + len(stages) - 1):
-            for depth in reversed(range(len(stages))):
-                jt = step - depth
-                if 0 <= jt < TILES:
-                    stages[depth](jt)
+        chunks = [(0, 1), (1, 2), (3, 2), (5, 2), (7, 1)]
+        stages = [
+            (quantise_hidden, 3),
+            (turn, 2),
+            (second_layer, 3),
+            (first_layer, 0),
+            (round_result, 4),
+            (quantise_result, 5),
+        ]
+        for jt in range(Y_BANKS):
+            first_pass(jt)
+        for step in range(len(chunks) + 5):
+            for stage, lag in stages:
+                if 0 <= step - lag < len(chunks):
+                    stage(*chunks[step - lag])
 
         for q in range(4):
             queue = nc.sync if q % 2 == 0 else nc.scalar

@@ -51,6 +51,9 @@ def tile_picked_zdq_mlprelu_po_kernel(
         w2_raw = keep.tile([P, N], I32, name="w2_raw")
         nc.sync.dma_start(w2_raw[:], w2_words[0].rearrange("p c b -> p (c b)").bitcast(I32))
 
+        w1_raw1 = first_space.tile([P, 4, H], F32, name="w1_raw1", offset=4 * T + 256)
+        nc.sync.dma_start(w1_raw1[:], w1_rows(1))
+
         zeros = first_space.tile([P, P], F32, name="zeros", offset=4 * T - 256)
         nc.vector.memset(zeros[:], 0.0)
         scale_table = scale_space.tile([P, T], U8, name="scale_table", offset=0)
@@ -68,8 +71,6 @@ def tile_picked_zdq_mlprelu_po_kernel(
         nc.vector.tensor_copy(ident[:], zeros[:])
         make_identity(nc, ident[:], nomemset=True)
 
-        w1_raw1 = first_space.tile([P, 4, H], F32, name="w1_raw1", offset=4 * T)
-        nc.sync.dma_start(w1_raw1[:], w1_rows(1))
         x_table0 = first_space.tile([P, T], I32, name="x_table0", offset=0)
         nc.sync.dma_start(x_table0[:], x_words[0].rearrange("p c b -> p (c b)").bitcast(I32))
 
@@ -95,7 +96,7 @@ def tile_picked_zdq_mlprelu_po_kernel(
         picked_scales = rows_space.tile([P, S], U8, name="picked_scales", offset=4 * S)
         nc.vector.tensor_copy(picked_scales[:], scale_table[:].indirect(offsets[:]))
 
-        queues = [[nc.scalar] * 4, [nc.sync] * 3 + [nc.gpsimd]]
+        queues = [[nc.sync] * 4, [nc.scalar] * 3 + [nc.gpsimd]]
         for o in range(PASSES):
             for q in range(4):
                 first = 4 * (16 * o + 4 * q)

@@ -22,7 +22,7 @@ RELU = mybir.ActivationFunctionType.Relu
 P = 128
 PASSES = K // 512
 TILES = S // P
-Y_BANKS = 3
+Y_BANKS = 6
 
 
 def tile_picked_zdq_mlprelu_po_kernel(
@@ -32,15 +32,21 @@ def tile_picked_zdq_mlprelu_po_kernel(
     with ExitStack() as ctx:
         keep = ctx.enter_context(tc.tile_pool(name="keep", bufs=1))
         ring = ctx.enter_context(tc.tile_pool(name="ring", bufs=3))
-        rows_space = ctx.enter_context(tc.tile_pool(name="rows_space", bufs=1))
         first_space = ctx.enter_context(tc.tile_pool(name="first_space", bufs=1))
         second_space = ctx.enter_context(tc.tile_pool(name="second_space", bufs=1))
         scale_space = ctx.enter_context(tc.tile_pool(name="scale_space", bufs=1))
-        psum = ctx.enter_context(tc.psum_pool(name="psum", bufs=2))
+        psum = ctx.enter_context(tc.psum_pool(name="psum", bufs=1))
 
         offsets = keep.tile([P, S // 16], U16, name="offsets")
         nc.sync.dma_start(offsets[:], offs)
-        wsum_cols = second_space.tile([P, 4], F32, name="wsum_cols", offset=0)
+
+        ident = keep.tile([P, P], F32, name="ident")
+        make_identity(nc, ident[:])
+
+        row_table = keep.tile([P, T], F32, name="row_table")
+        nc.sync.dma_start(row_table[P - 2 : P - 1, :], gain[0:1, :])
+        nc.sync.dma_start(row_table[P - 1 : P, :], shift[0:1, :])
+        wsum_cols = keep.tile([P, 4], F32, name="wsum_cols")
         nc.scalar.dma_start(wsum_cols[:], wsum.rearrange("(p t) o -> p (t o)", t=4))
 
         def w1_rows(o):
@@ -50,33 +56,19 @@ def tile_picked_zdq_mlprelu_po_kernel(
         nc.sync.dma_start(w1_raw0[:], w1_rows(0))
         w2_raw = keep.tile([P, N], I32, name="w2_raw")
         nc.sync.dma_start(w2_raw[:], w2_words[0].rearrange("p c b -> p (c b)").bitcast(I32))
-
-        w1_raw1 = first_space.tile([P, 4, H], F32, name="w1_raw1", offset=4 * T + 256)
+        w1_raw1 = second_space.tile([P, 4, H], F32, name="w1_raw1", offset=0)
         nc.sync.dma_start(w1_raw1[:], w1_rows(1))
 
-        zeros = first_space.tile([P, P], F32, name="zeros", offset=4 * T - 256)
-        nc.vector.memset(zeros[:], 0.0)
         scale_table = scale_space.tile([P, T], U8, name="scale_table", offset=0)
         nc.vector.memset(scale_table[:].bitcast(I32), 0)
-        nc.scalar.dma_start(scale_table[0:P:4, :].bitcast(I32), x_scales.rearrange("o q c -> (o q) c").bitcast(I32))
+        nc.gpsimd.dma_start(scale_table[96:104, :].bitcast(I32), x_scales[:, 12:16, :].bitcast(I32))
+        for q in range(3):
+            for o in range(PASSES):
+                nc.sync.dma_start(
+                    scale_table[32 * q + 4 * o : 32 * q + 4 * o + 4, :].bitcast(I32),
+                    x_scales[o, 4 * q : 4 * q + 4, :].bitcast(I32),
+                )
 
-        row_table = rows_space.tile([P, T], F32, name="row_table", offset=0)
-        nc.vector.tensor_copy(
-            row_table[:].rearrange("p (a b) -> p a b", b=P), zeros[:].unsqueeze(1).to_broadcast([P, T // P, P])
-        )
-        nc.sync.dma_start(row_table[0:1, :], gain[0:1, :])
-        nc.sync.dma_start(row_table[64:65, :], shift[0:1, :])
-
-        ident = keep.tile([P, P], F32, name="ident")
-        nc.vector.tensor_copy(ident[:], zeros[:])
-        make_identity(nc, ident[:], nomemset=True)
-
-        x_table0 = first_space.tile([P, T], I32, name="x_table0", offset=0)
-        nc.sync.dma_start(x_table0[:], x_words[0].rearrange("p c b -> p (c b)").bitcast(I32))
-
-        x_planes = [keep.tile([P, S], U8, name="x_plane%d" % o, align_bytes=64) for o in range(PASSES)]
-        for plane in x_planes:
-            nc.vector.memset(plane[:].bitcast(I32), 0)
         w2_raw_scales = keep.tile([P, N], U8, name="w2_raw_scales")
         nc.vector.memset(w2_raw_scales[:].bitcast(I32), 0)
         for q in range(4):
@@ -84,34 +76,38 @@ def tile_picked_zdq_mlprelu_po_kernel(
                 w2_raw_scales[32 * q : 32 * q + 4, :].bitcast(I32), w2_scales[0, 4 * q : 4 * q + 4, :].bitcast(I32)
             )
 
-        wsum_rows = psum.tile([P, 4, P], F32, name="wsum_rows", tag="result", bufs=3)
+        zeros = first_space.tile([P, P], F32, name="zeros", offset=4 * T - 256)
+        nc.vector.memset(zeros[:], 0.0)
+        nc.vector.tensor_copy(
+            row_table[0 : P - 2, :].rearrange("p (a b) -> p a b", b=P),
+            zeros[0 : P - 2, :].unsqueeze(1).to_broadcast([P - 2, T // P, P]),
+        )
+
+        x_table0 = first_space.tile([P, T], I32, name="x_table0", offset=0)
+        nc.sync.dma_start(x_table0[:], x_words[0].rearrange("p c b -> p (c b)").bitcast(I32))
+        x_table1 = first_space.tile([P, T], I32, name="x_table1", offset=4 * T)
+        nc.sync.dma_start(x_table1[:], x_words[1].rearrange("p c b -> p (c b)").bitcast(I32))
+
+        def bank(b, shape):
+            return psum.tile(shape, F32, name="bank%d" % b, tag="bank%d" % b)
+
+        wsum_rows = bank(5, [P, 4, P])
         for t in range(4):
             nc.tensor.transpose(wsum_rows[:, t, :], wsum_cols[:, t : t + 1].to_broadcast([P, P]), ident[:])
 
-        x_table1 = second_space.tile([P, T], I32, name="x_table1", offset=0)
-        nc.sync.dma_start(x_table1[:], x_words[1].rearrange("p c b -> p (c b)").bitcast(I32))
-
         picked_rows = keep.tile([P, S], F32, name="picked_rows")
         nc.vector.tensor_copy(picked_rows[:], row_table[:].indirect(offsets[:]))
-        picked_scales = rows_space.tile([P, S], U8, name="picked_scales", offset=4 * S)
-        nc.vector.tensor_copy(picked_scales[:], scale_table[:].indirect(offsets[:]))
-
-        queues = [[nc.sync] * 4, [nc.scalar] * 3 + [nc.gpsimd]]
-        for o in range(PASSES):
-            for q in range(4):
-                first = 4 * (16 * o + 4 * q)
-                queues[o][q].dma_start(
-                    x_planes[o][32 * q : 32 * q + 4, :].bitcast(I32),
-                    picked_scales[first : first + 16 : 4, :].bitcast(I32),
-                )
-
-        x_code0 = scale_space.tile([P, S], U32, name="x_code0", align_bytes=64, offset=0)
-        nc.vector.tensor_copy(x_code0[:], x_table0[:].bitcast(U32).indirect(offsets[:]))
+        x_plane = keep.tile([P, S], U8, name="x_plane", align_bytes=64)
+        nc.vector.tensor_copy(x_plane[:], scale_table[:].indirect(offsets[:]))
 
         w2_codes = keep.tile([P, N], I32, name="w2_codes", align_bytes=64)
         nc.vector.tensor_copy(
             w2_codes[:].rearrange("p (t m) -> p t m", t=4), w2_raw[:].rearrange("p (m t) -> p t m", t=4)
         )
+
+        x_code0 = scale_space.tile([P, S], U32, name="x_code0", align_bytes=64, offset=0)
+        nc.vector.tensor_copy(x_code0[:], x_table0[:].bitcast(U32).indirect(offsets[:]))
+
         w2_plane = first_space.tile([P, N], U8, name="w2_plane", align_bytes=64, offset=0)
         nc.vector.tensor_copy(
             w2_plane[:].rearrange("p (t m) -> p t m", t=4), w2_raw_scales[:].rearrange("p (m t) -> p t m", t=4)
@@ -136,13 +132,13 @@ def tile_picked_zdq_mlprelu_po_kernel(
             w1_codes.append(codes)
             w1_plane.append(plane)
 
-        factors = first_space.tile([P, TILES, 2], F32, name="factors", offset=4 * T + 256)
+        factors = second_space.tile([P, TILES, 2], F32, name="factors", offset=0)
         for b in range(2):
-            turned = psum.tile([P, 4, P], F32, name="turned", tag="turn")
+            turned = bank(6 + b, [P, 4, P])
             for a in range(4):
                 jt = 4 * b + a
                 nc.tensor.transpose(turned[:, a, :], picked_rows[:, P * jt : P * (jt + 1)], ident[:])
-            nc.scalar.copy(factors[:, 4 * b : 4 * b + 4, :], turned[:, :, 0:P:64])
+            nc.scalar.copy(factors[:, 4 * b : 4 * b + 4, :], turned[:, :, P - 2 : P])
 
         offsets_term = []
         for jt in range(TILES):
@@ -166,11 +162,11 @@ def tile_picked_zdq_mlprelu_po_kernel(
 
         def first_pass(jt):
             cols = slice(P * jt, P * (jt + 1))
-            y = psum.tile([P, H], F32, name="y", bufs=Y_BANKS)
+            y = bank(jt % Y_BANKS, [P, H])
             nc.tensor.matmul_mx(
                 out=y[:],
                 lhsT=x_code0[:, cols].bitcast(FP8X4),
-                lhsT_scale=x_planes[0][:, cols],
+                lhsT_scale=x_plane[:, cols],
                 rhs=w1_codes[0][:].bitcast(FP8X4),
                 rhs_scale=w1_plane[0][:],
                 start=True,
@@ -186,7 +182,7 @@ def tile_picked_zdq_mlprelu_po_kernel(
                 nc.tensor.matmul_mx(
                     out=sums[jt][:],
                     lhsT=x_code1[half][:, P * place : P * (place + 1)].bitcast(FP8X4),
-                    lhsT_scale=x_planes[1][:, P * jt : P * (jt + 1)],
+                    lhsT_scale=x_plane[4:P, P * jt : P * (jt + 1)],
                     rhs=w1_codes[1][:].bitcast(FP8X4),
                     rhs_scale=w1_plane[1][:],
                     start=False,
@@ -203,7 +199,7 @@ def tile_picked_zdq_mlprelu_po_kernel(
 
         def turn(first, count):
             n = P * count
-            turned = psum.tile([P, 2, n], F32, name="turned_pairs", tag="turn")
+            turned = bank(6 + (first + 1) // 2 % 2, [P, 2, n])
             for a in range(count):
                 words = pre[first + a][:].bitcast(F32)
                 for u in range(2):
@@ -228,10 +224,10 @@ def tile_picked_zdq_mlprelu_po_kernel(
             codes, plane = hidden_mx[first]
             res = keep.tile([P, 4, n], F32, name="res%d" % first)
             per_bank = 4 // count
-            for bank in range(count):
-                acc = psum.tile([P, per_bank, n], F32, name="acc", tag="result", bufs=3)
+            for part in range(count):
+                acc = bank((2 + first + part) % Y_BANKS, [P, per_bank, n])
                 for s in range(per_bank):
-                    t = per_bank * bank + s
+                    t = per_bank * part + s
                     nc.tensor.matmul_mx(
                         out=acc[:, s, :],
                         lhsT=w2_codes[:, P * t : P * (t + 1)].bitcast(FP8X4),
@@ -241,7 +237,7 @@ def tile_picked_zdq_mlprelu_po_kernel(
                         start=True,
                         stop=True,
                     )
-                nc.scalar.copy(res[:, per_bank * bank : per_bank * (bank + 1), :], acc[:])
+                nc.scalar.copy(res[:, per_bank * part : per_bank * (part + 1), :], acc[:])
             nc.sync.dma_start(out_rows[:, :, P * first : P * first + n], res[:])
             result[first] = res
 
@@ -261,10 +257,10 @@ def tile_picked_zdq_mlprelu_po_kernel(
 
         chunks = [(0, 1), (1, 2), (3, 2), (5, 2), (7, 1)]
         stages = [
-            (quantise_hidden, 3),
-            (turn, 2),
-            (second_layer, 3),
             (first_layer, 0),
+            (turn, 1),
+            (quantise_hidden, 2),
+            (second_layer, 2),
             (round_result, 4),
             (quantise_result, 5),
         ]

@@ -23,6 +23,7 @@ P = 128
 PASSES = K // 512
 TILES = S // P
 Y_BANKS = 6
+EARLY = 4
 
 
 def tile_picked_zdq_mlprelu_po_kernel(
@@ -33,8 +34,8 @@ def tile_picked_zdq_mlprelu_po_kernel(
         keep = ctx.enter_context(tc.tile_pool(name="keep", bufs=1))
         ring = ctx.enter_context(tc.tile_pool(name="ring", bufs=3))
         first_space = ctx.enter_context(tc.tile_pool(name="first_space", bufs=1))
-        second_space = ctx.enter_context(tc.tile_pool(name="second_space", bufs=1))
         scale_space = ctx.enter_context(tc.tile_pool(name="scale_space", bufs=1))
+        second_space = ctx.enter_context(tc.tile_pool(name="second_space", bufs=1))
         psum = ctx.enter_context(tc.psum_pool(name="psum", bufs=1))
 
         offsets = keep.tile([P, S // 16], U16, name="offsets")
@@ -52,22 +53,24 @@ def tile_picked_zdq_mlprelu_po_kernel(
         def w1_rows(o):
             return w1[512 * o : 512 * (o + 1), :].rearrange("(p j) c -> p j c", j=4)
 
-        w1_raw0 = keep.tile([P, 4, H], F32, name="w1_raw0")
-        nc.sync.dma_start(w1_raw0[:], w1_rows(0))
         w2_raw = keep.tile([P, N], I32, name="w2_raw")
         nc.sync.dma_start(w2_raw[:], w2_words[0].rearrange("p c b -> p (c b)").bitcast(I32))
-        w1_raw1 = second_space.tile([P, 4, H], F32, name="w1_raw1", offset=0)
+        w1_raw1 = first_space.tile([P, 4, H], F32, name="w1_raw1", offset=4 * T)
         nc.sync.dma_start(w1_raw1[:], w1_rows(1))
 
         scale_table = scale_space.tile([P, T], U8, name="scale_table", offset=0)
-        nc.vector.memset(scale_table[:].bitcast(I32), 0)
-        nc.gpsimd.dma_start(scale_table[96:104, :].bitcast(I32), x_scales[:, 12:16, :].bitcast(I32))
-        for q in range(3):
+
+        def load_scale_rows(q):
             for o in range(PASSES):
                 nc.sync.dma_start(
                     scale_table[32 * q + 4 * o : 32 * q + 4 * o + 4, :].bitcast(I32),
                     x_scales[o, 4 * q : 4 * q + 4, :].bitcast(I32),
                 )
+
+        nc.vector.memset(scale_table[:].bitcast(I32), 0)
+        nc.gpsimd.dma_start(scale_table[96:104, :].bitcast(I32), x_scales[:, 12:16, :].bitcast(I32))
+        for q in range(3):
+            load_scale_rows(q)
 
         w2_raw_scales = keep.tile([P, N], U8, name="w2_raw_scales")
         nc.vector.memset(w2_raw_scales[:].bitcast(I32), 0)
@@ -76,17 +79,32 @@ def tile_picked_zdq_mlprelu_po_kernel(
                 w2_raw_scales[32 * q : 32 * q + 4, :].bitcast(I32), w2_scales[0, 4 * q : 4 * q + 4, :].bitcast(I32)
             )
 
-        zeros = first_space.tile([P, P], F32, name="zeros", offset=4 * T - 256)
-        nc.vector.memset(zeros[:], 0.0)
-        nc.vector.tensor_copy(
-            row_table[0 : P - 2, :].rearrange("p (a b) -> p a b", b=P),
-            zeros[0 : P - 2, :].unsqueeze(1).to_broadcast([P - 2, T // P, P]),
-        )
+        zeros = [
+            first_space.tile([P, 64], F32, name="zeros0", offset=4 * T - 256),
+            second_space.tile([P, 64], F32, name="zeros1", offset=4 * T - 128),
+            second_space.tile([P, 64], F32, name="zeros2", offset=4 * T + 8 * H),
+        ]
+        for source in zeros:
+            nc.vector.memset(source[:], 0.0)
 
+        def fill_rows(first, width, source):
+            nc.vector.tensor_copy(
+                row_table[0 : P - 2, first : first + width].rearrange("p (a b) -> p a b", b=64),
+                source[0 : P - 2, :].unsqueeze(1).to_broadcast([P - 2, width // 64, 64]),
+            )
+
+        fill_rows(0, T // 2, zeros[0])
         x_table0 = first_space.tile([P, T], I32, name="x_table0", offset=0)
         nc.sync.dma_start(x_table0[:], x_words[0].rearrange("p c b -> p (c b)").bitcast(I32))
-        x_table1 = first_space.tile([P, T], I32, name="x_table1", offset=4 * T)
+        fill_rows(T // 2, T // 4, zeros[1])
+        fill_rows(3 * T // 4, T // 4, zeros[2])
+        x_table1 = second_space.tile([P, T], I32, name="x_table1", offset=0)
         nc.sync.dma_start(x_table1[:], x_words[1].rearrange("p c b -> p (c b)").bitcast(I32))
+        w1_raw0 = []
+        for half in range(2):
+            raw = second_space.tile([P, 4, H // 2], F32, name="w1_raw0%d" % half, offset=4 * T + 8 * H * half)
+            nc.sync.dma_start(raw[:], w1_rows(0)[:, :, H // 2 * half : H // 2 * (half + 1)])
+            w1_raw0.append(raw)
 
         def bank(b, shape):
             return psum.tile(shape, F32, name="bank%d" % b, tag="bank%d" % b)
@@ -97,42 +115,23 @@ def tile_picked_zdq_mlprelu_po_kernel(
 
         picked_rows = keep.tile([P, S], F32, name="picked_rows")
         nc.vector.tensor_copy(picked_rows[:], row_table[:].indirect(offsets[:]))
-        x_plane = keep.tile([P, S], U8, name="x_plane", align_bytes=64)
-        nc.vector.tensor_copy(x_plane[:], scale_table[:].indirect(offsets[:]))
 
         w2_codes = keep.tile([P, N], I32, name="w2_codes", align_bytes=64)
         nc.vector.tensor_copy(
             w2_codes[:].rearrange("p (t m) -> p t m", t=4), w2_raw[:].rearrange("p (m t) -> p t m", t=4)
         )
 
+        x_plane = keep.tile([P, S], U8, name="x_plane", align_bytes=64)
+        nc.vector.tensor_copy(x_plane[:], scale_table[:].indirect(offsets[:]))
         x_code0 = scale_space.tile([P, S], U32, name="x_code0", align_bytes=64, offset=0)
         nc.vector.tensor_copy(x_code0[:], x_table0[:].bitcast(U32).indirect(offsets[:]))
 
-        w2_plane = first_space.tile([P, N], U8, name="w2_plane", align_bytes=64, offset=0)
-        nc.vector.tensor_copy(
+        w2_plane = keep.tile([P, N], U8, name="w2_plane", align_bytes=64)
+        nc.gpsimd.tensor_copy(
             w2_plane[:].rearrange("p (t m) -> p t m", t=4), w2_raw_scales[:].rearrange("p (m t) -> p t m", t=4)
         )
 
-        x_code1 = [keep.tile([P, S // 2], U32, name="x_code1%d" % half, align_bytes=64) for half in range(2)]
-        for half in range(2):
-            nc.vector.tensor_copy(
-                x_code1[half][:], x_table1[:].bitcast(U32).indirect(offsets[:, S // 32 * half : S // 32 * (half + 1)])
-            )
-
-        w1_codes, w1_plane = [], []
-        for o, raw in enumerate([w1_raw0, w1_raw1]):
-            g = keep.tile([P, 4 * H], BF16, name="w1_grouped%d" % o, align_bytes=64)
-            nc.scalar.copy(
-                g[:].rearrange("p (u m e j) -> p u m j e", u=2, e=2, j=4),
-                raw[:].rearrange("p j (m u e) -> p u m j e", u=2, e=2),
-            )
-            codes = keep.tile([P, H], U32, name="w1_codes%d" % o, align_bytes=64)
-            plane = keep.tile([P, H], U8, name="w1_plane%d" % o, align_bytes=64)
-            nc.vector.quantize_mx(out=codes[:].bitcast(FP8X4), scales=plane[:], in_=g[:])
-            w1_codes.append(codes)
-            w1_plane.append(plane)
-
-        factors = second_space.tile([P, TILES, 2], F32, name="factors", offset=0)
+        factors = first_space.tile([P, TILES, 2], F32, name="factors", offset=4 * T)
         for b in range(2):
             turned = bank(6 + b, [P, 4, P])
             for a in range(4):
@@ -151,7 +150,38 @@ def tile_picked_zdq_mlprelu_po_kernel(
             )
             offsets_term.append(term)
 
+        w1_codes = [keep.tile([P, H], U32, name="w1_codes%d" % o, align_bytes=64) for o in range(PASSES)]
+        w1_plane = [keep.tile([P, H], U8, name="w1_plane%d" % o, align_bytes=64) for o in range(PASSES)]
+        g = keep.tile([P, 4 * H], BF16, name="w1_grouped1", align_bytes=64)
+        nc.scalar.copy(
+            g[:].rearrange("p (u m e j) -> p u m j e", u=2, e=2, j=4),
+            w1_raw1[:].rearrange("p j (m u e) -> p u m j e", u=2, e=2),
+        )
+        nc.vector.quantize_mx(out=w1_codes[1][:].bitcast(FP8X4), scales=w1_plane[1][:], in_=g[:])
+
+        x_code1 = [keep.tile([P, S // 2], U32, name="x_code1%d" % half, align_bytes=64) for half in range(2)]
+        for half in range(2):
+            nc.vector.tensor_copy(
+                x_code1[half][:], x_table1[:].bitcast(U32).indirect(offsets[:, S // 32 * half : S // 32 * (half + 1)])
+            )
+
+        for half in range(2):
+            pieces = []
+            for u in range(2):
+                g = keep.tile([P, H], BF16, name="w1_grouped0%d%d" % (half, u), align_bytes=64)
+                copy = nc.vector.tensor_copy if (half, u) == (1, 1) else nc.scalar.copy
+                copy(
+                    g[:].rearrange("p (m e j) -> p m j e", e=2, j=4),
+                    w1_raw0[half][:].rearrange("p j (m u e) -> p u m j e", u=2, e=2)[:, u],
+                )
+                pieces.append(g)
+            for u in range(2):
+                cols = slice(H // 2 * u + H // 4 * half, H // 2 * u + H // 4 * (half + 1))
+                nc.vector.quantize_mx(out=w1_codes[0][:, cols].bitcast(FP8X4), scales=w1_plane[0][:, cols], in_=pieces[u][:])
+
         out_plane = keep.tile([P, S], U8, name="out_plane", align_bytes=64)
+        out_codes = keep.tile([P, S], U32, name="out_codes", align_bytes=64)
+        word_stores = {1: 0, 5: 3, 7: 7}
         out_rows = out_0.rearrange("(p t) j -> p t j", t=4)
         out_words = out_1[0].rearrange("p c b -> p (c b)").bitcast(I32)
 
@@ -160,34 +190,28 @@ def tile_picked_zdq_mlprelu_po_kernel(
 
         sums = {}
 
-        def first_pass(jt):
+        def product_pass(jt, o):
+            half, place = divmod(jt, TILES // 2)
             cols = slice(P * jt, P * (jt + 1))
-            y = bank(jt % Y_BANKS, [P, H])
+            opens = jt not in sums
+            if opens:
+                sums[jt] = bank(jt % Y_BANKS, [P, H])
+            codes = x_code0[:, cols] if o == 0 else x_code1[half][:, P * place : P * (place + 1)]
             nc.tensor.matmul_mx(
-                out=y[:],
-                lhsT=x_code0[:, cols].bitcast(FP8X4),
-                lhsT_scale=x_plane[:, cols],
-                rhs=w1_codes[0][:].bitcast(FP8X4),
-                rhs_scale=w1_plane[0][:],
-                start=True,
-                stop=False,
+                out=sums[jt][:],
+                lhsT=codes.bitcast(FP8X4),
+                lhsT_scale=x_plane[4 * o : P, cols],
+                rhs=w1_codes[o][:].bitcast(FP8X4),
+                rhs_scale=w1_plane[o][:],
+                start=opens,
+                stop=not opens,
             )
-            sums[jt] = y
 
         def first_layer(first, count):
             for jt in range(first, first + count):
-                if jt not in sums:
-                    first_pass(jt)
-                half, place = divmod(jt, TILES // 2)
-                nc.tensor.matmul_mx(
-                    out=sums[jt][:],
-                    lhsT=x_code1[half][:, P * place : P * (place + 1)].bitcast(FP8X4),
-                    lhsT_scale=x_plane[4:P, P * jt : P * (jt + 1)],
-                    rhs=w1_codes[1][:].bitcast(FP8X4),
-                    rhs_scale=w1_plane[1][:],
-                    start=False,
-                    stop=True,
-                )
+                product_pass(jt, 0)
+                if jt >= EARLY:
+                    product_pass(jt, 1)
                 nc.vector.scalar_tensor_tensor(
                     out=pre[jt][:],
                     in0=sums[jt][:],
@@ -205,11 +229,12 @@ def tile_picked_zdq_mlprelu_po_kernel(
                 for u in range(2):
                     nc.tensor.transpose(turned[:, u, P * a : P * (a + 1)], words[:, P * u : P * (u + 1)], ident[:])
             h = ring.tile([P, 4 * n], BF16, name="h", align_bytes=64)
-            nc.scalar.activation(
-                h[:].rearrange("p (j u e) -> p j u e", u=2, e=2),
-                turned[:].bitcast(BF16).rearrange("p u (j e) -> p j u e", e=2),
-                RELU,
-            )
+            pairs_out = h[:].rearrange("p (j u e) -> p j u e", u=2, e=2)
+            pairs_in = turned[:].bitcast(BF16).rearrange("p u (j e) -> p j u e", e=2)
+            if first == 5:
+                nc.vector.tensor_scalar_max(pairs_out, pairs_in, 0.0)
+            else:
+                nc.scalar.activation(pairs_out, pairs_in, RELU)
             hidden[first] = h
 
         def quantise_hidden(first, count):
@@ -251,9 +276,10 @@ def tile_picked_zdq_mlprelu_po_kernel(
 
         def quantise_result(first, count):
             cols = slice(P * first, P * (first + count))
-            codes = keep.tile([P, P * count], U32, name="out_codes%d" % first, align_bytes=64)
-            nc.vector.quantize_mx(out=codes[:].bitcast(FP8X4), scales=out_plane[:, cols], in_=rounded[first][:])
-            nc.sync.dma_start(out_words[:, cols], codes[:].bitcast(I32))
+            nc.vector.quantize_mx(out=out_codes[:, cols].bitcast(FP8X4), scales=out_plane[:, cols], in_=rounded[first][:])
+            if first in word_stores:
+                done = slice(P * word_stores[first], P * (first + count))
+                nc.sync.dma_start(out_words[:, done], out_codes[:, done].bitcast(I32))
 
         chunks = [(0, 1), (1, 2), (3, 2), (5, 2), (7, 1)]
         stages = [
@@ -264,8 +290,8 @@ def tile_picked_zdq_mlprelu_po_kernel(
             (round_result, 4),
             (quantise_result, 5),
         ]
-        for jt in range(Y_BANKS):
-            first_pass(jt)
+        for jt in range(EARLY):
+            product_pass(jt, 1)
         for step in range(len(chunks) + 5):
             for stage, lag in stages:
                 if 0 <= step - lag < len(chunks):

@@ -43,68 +43,40 @@ def tile_picked_zdq_mlprelu_po_kernel(
 
         ident = keep.tile([P, P], F32, name="ident")
         make_identity(nc, ident[:])
-
-        row_table = keep.tile([P, T], F32, name="row_table")
-        nc.sync.dma_start(row_table[P - 2 : P - 1, :], gain[0:1, :])
-        nc.sync.dma_start(row_table[P - 1 : P, :], shift[0:1, :])
         wsum_cols = keep.tile([P, 4], F32, name="wsum_cols")
         nc.scalar.dma_start(wsum_cols[:], wsum.rearrange("(p t) o -> p (t o)", t=4))
 
         def w1_rows(o):
             return w1[512 * o : 512 * (o + 1), :].rearrange("(p j) c -> p j c", j=4)
 
-        w2_raw = keep.tile([P, N], I32, name="w2_raw")
+        w2_raw = second_space.tile([P, N], I32, name="w2_raw", offset=4 * T - 2 * N)
         nc.sync.dma_start(w2_raw[:], w2_words[0].rearrange("p c b -> p (c b)").bitcast(I32))
         w1_raw1 = first_space.tile([P, 4, H], F32, name="w1_raw1", offset=4 * T)
         nc.sync.dma_start(w1_raw1[:], w1_rows(1))
 
         scale_table = scale_space.tile([P, T], U8, name="scale_table", offset=0)
-
-        def load_scale_rows(q):
-            for o in range(PASSES):
-                nc.sync.dma_start(
-                    scale_table[32 * q + 4 * o : 32 * q + 4 * o + 4, :].bitcast(I32),
-                    x_scales[o, 4 * q : 4 * q + 4, :].bitcast(I32),
-                )
-
         nc.vector.memset(scale_table[:].bitcast(I32), 0)
-        nc.gpsimd.dma_start(scale_table[96:104, :].bitcast(I32), x_scales[:, 12:16, :].bitcast(I32))
-        for q in range(3):
-            load_scale_rows(q)
+        for o in range(PASSES):
+            nc.scalar.dma_start(scale_table[4 * o : P : 8, :].bitcast(I32), x_scales[o].bitcast(I32))
 
         w2_raw_scales = keep.tile([P, N], U8, name="w2_raw_scales")
-        nc.vector.memset(w2_raw_scales[:].bitcast(I32), 0)
+        nc.gpsimd.memset(w2_raw_scales[:].bitcast(I32), 0)
         for q in range(4):
             nc.gpsimd.dma_start(
                 w2_raw_scales[32 * q : 32 * q + 4, :].bitcast(I32), w2_scales[0, 4 * q : 4 * q + 4, :].bitcast(I32)
             )
 
-        zeros = [
-            first_space.tile([P, 64], F32, name="zeros0", offset=4 * T - 256),
-            second_space.tile([P, 64], F32, name="zeros1", offset=4 * T - 128),
-            second_space.tile([P, 64], F32, name="zeros2", offset=4 * T + 8 * H),
-        ]
-        for source in zeros:
-            nc.vector.memset(source[:], 0.0)
+        zeros = first_space.tile([P, P], F32, name="zeros", offset=4 * T - 4 * P)
+        nc.vector.memset(zeros[:], 0.0)
+        row_table = keep.tile([P, T], F32, name="row_table")
+        nc.vector.tensor_copy(
+            row_table[:].rearrange("p (a b) -> p a b", b=P), zeros[:].unsqueeze(1).to_broadcast([P, T // P, P])
+        )
+        nc.sync.dma_start(row_table[0:1, :], gain[0:1, :])
+        nc.sync.dma_start(row_table[64:65, :], shift[0:1, :])
 
-        def fill_rows(first, width, source):
-            nc.vector.tensor_copy(
-                row_table[0 : P - 2, first : first + width].rearrange("p (a b) -> p a b", b=64),
-                source[0 : P - 2, :].unsqueeze(1).to_broadcast([P - 2, width // 64, 64]),
-            )
-
-        fill_rows(0, T // 2, zeros[0])
         x_table0 = first_space.tile([P, T], I32, name="x_table0", offset=0)
         nc.sync.dma_start(x_table0[:], x_words[0].rearrange("p c b -> p (c b)").bitcast(I32))
-        fill_rows(T // 2, T // 4, zeros[1])
-        fill_rows(3 * T // 4, T // 4, zeros[2])
-        x_table1 = second_space.tile([P, T], I32, name="x_table1", offset=0)
-        nc.sync.dma_start(x_table1[:], x_words[1].rearrange("p c b -> p (c b)").bitcast(I32))
-        w1_raw0 = []
-        for half in range(2):
-            raw = second_space.tile([P, 4, H // 2], F32, name="w1_raw0%d" % half, offset=4 * T + 8 * H * half)
-            nc.sync.dma_start(raw[:], w1_rows(0)[:, :, H // 2 * half : H // 2 * (half + 1)])
-            w1_raw0.append(raw)
 
         def bank(b, shape):
             return psum.tile(shape, F32, name="bank%d" % b, tag="bank%d" % b)
@@ -113,17 +85,31 @@ def tile_picked_zdq_mlprelu_po_kernel(
         for t in range(4):
             nc.tensor.transpose(wsum_rows[:, t, :], wsum_cols[:, t : t + 1].to_broadcast([P, P]), ident[:])
 
-        picked_rows = keep.tile([P, S], F32, name="picked_rows")
-        nc.vector.tensor_copy(picked_rows[:], row_table[:].indirect(offsets[:]))
+        picked_scales = keep.tile([P, S], U8, name="picked_scales")
+        nc.vector.tensor_copy(picked_scales[:], scale_table[:].indirect(offsets[:]))
+        x_plane = keep.tile([P, S], U8, name="x_plane", align_bytes=64)
+        nc.vector.tensor_copy(x_plane[:].bitcast(I32), picked_scales[:].bitcast(I32))
+        for o in reversed(range(PASSES)):
+            for r in range(1, 4):
+                nc.sync.dma_start(
+                    x_plane[4 * o + r : P : 32, :].bitcast(I32), picked_scales[8 * r + 4 * o : P : 32, :].bitcast(I32)
+                )
 
-        w2_codes = keep.tile([P, N], I32, name="w2_codes", align_bytes=64)
+        w2_codes = scale_space.tile([P, N], I32, name="w2_codes", align_bytes=64, offset=0)
         nc.vector.tensor_copy(
             w2_codes[:].rearrange("p (t m) -> p t m", t=4), w2_raw[:].rearrange("p (m t) -> p t m", t=4)
         )
 
-        x_plane = keep.tile([P, S], U8, name="x_plane", align_bytes=64)
-        nc.vector.tensor_copy(x_plane[:], scale_table[:].indirect(offsets[:]))
-        x_code0 = scale_space.tile([P, S], U32, name="x_code0", align_bytes=64, offset=0)
+        x_table1 = second_space.tile([P, T], I32, name="x_table1", offset=0)
+        nc.sync.dma_start(x_table1[:], x_words[1].rearrange("p c b -> p (c b)").bitcast(I32))
+        w1_raw0 = second_space.tile([P, 2, 4, H // 2], F32, name="w1_raw0", offset=4 * T)
+        for half in range(2):
+            nc.sync.dma_start(w1_raw0[:, half], w1_rows(0)[:, :, H // 2 * half : H // 2 * (half + 1)])
+
+        picked_rows = keep.tile([P, S], F32, name="picked_rows")
+        nc.vector.tensor_copy(picked_rows[:], row_table[:].indirect(offsets[:]))
+
+        x_code0 = keep.tile([P, S], U32, name="x_code0", align_bytes=64)
         nc.vector.tensor_copy(x_code0[:], x_table0[:].bitcast(U32).indirect(offsets[:]))
 
         w2_plane = keep.tile([P, N], U8, name="w2_plane", align_bytes=64)
@@ -137,7 +123,7 @@ def tile_picked_zdq_mlprelu_po_kernel(
             for a in range(4):
                 jt = 4 * b + a
                 nc.tensor.transpose(turned[:, a, :], picked_rows[:, P * jt : P * (jt + 1)], ident[:])
-            nc.scalar.copy(factors[:, 4 * b : 4 * b + 4, :], turned[:, :, P - 2 : P])
+            nc.scalar.copy(factors[:, 4 * b : 4 * b + 4, :], turned[:, :, 0:P:64])
 
         offsets_term = []
         for jt in range(TILES):
@@ -172,7 +158,7 @@ def tile_picked_zdq_mlprelu_po_kernel(
                 copy = nc.vector.tensor_copy if (half, u) == (1, 1) else nc.scalar.copy
                 copy(
                     g[:].rearrange("p (m e j) -> p m j e", e=2, j=4),
-                    w1_raw0[half][:].rearrange("p j (m u e) -> p u m j e", u=2, e=2)[:, u],
+                    w1_raw0[:, half].rearrange("p j (m u e) -> p u m j e", u=2, e=2)[:, u],
                 )
                 pieces.append(g)
             for u in range(2):

@@ -23,7 +23,7 @@ P = 128
 PASSES = K // 512
 TILES = S // P
 Y_BANKS = 6
-EARLY = 4
+EARLY = 6
 
 
 def tile_picked_zdq_mlprelu_po_kernel(
@@ -43,21 +43,25 @@ def tile_picked_zdq_mlprelu_po_kernel(
 
         ident = keep.tile([P, P], F32, name="ident")
         make_identity(nc, ident[:])
+        row_table = keep.tile([P, T], F32, name="row_table")
+        nc.sync.dma_start(row_table[P - 2 : P - 1, :], gain[0:1, :])
+        nc.sync.dma_start(row_table[P - 1 : P, :], shift[0:1, :])
         wsum_cols = keep.tile([P, 4], F32, name="wsum_cols")
         nc.scalar.dma_start(wsum_cols[:], wsum.rearrange("(p t) o -> p (t o)", t=4))
 
         def w1_rows(o):
             return w1[512 * o : 512 * (o + 1), :].rearrange("(p j) c -> p j c", j=4)
 
-        w2_raw = second_space.tile([P, N], I32, name="w2_raw", offset=4 * T - 2 * N)
-        nc.sync.dma_start(w2_raw[:], w2_words[0].rearrange("p c b -> p (c b)").bitcast(I32))
-        w1_raw1 = first_space.tile([P, 4, H], F32, name="w1_raw1", offset=4 * T)
-        nc.sync.dma_start(w1_raw1[:], w1_rows(1))
+        w1_raw0 = keep.tile([P, 4, H], F32, name="w1_raw0")
+        nc.sync.dma_start(w1_raw0[:], w1_rows(0))
+
+        first_zeros = second_space.tile([P, P], F32, name="first_zeros", offset=4 * T + 2 * N - 2 * P)
+        nc.vector.memset(first_zeros[:], 0.0)
 
         scale_table = scale_space.tile([P, T], U8, name="scale_table", offset=0)
         nc.vector.memset(scale_table[:].bitcast(I32), 0)
         for o in range(PASSES):
-            nc.scalar.dma_start(scale_table[4 * o : P : 8, :].bitcast(I32), x_scales[o].bitcast(I32))
+            nc.sync.dma_start(scale_table[4 * o : P : 8, :].bitcast(I32), x_scales[o].bitcast(I32))
 
         w2_raw_scales = keep.tile([P, N], U8, name="w2_raw_scales")
         nc.gpsimd.memset(w2_raw_scales[:].bitcast(I32), 0)
@@ -67,13 +71,15 @@ def tile_picked_zdq_mlprelu_po_kernel(
             )
 
         zeros = first_space.tile([P, P], F32, name="zeros", offset=4 * T - 4 * P)
-        nc.vector.memset(zeros[:], 0.0)
-        row_table = keep.tile([P, T], F32, name="row_table")
+        nc.vector.tensor_copy(zeros[:], first_zeros[:])
+        w2_raw = second_space.tile([P, N], I32, name="w2_raw", offset=4 * T - 2 * N)
+        nc.sync.dma_start(w2_raw[:], w2_words[0].rearrange("p c b -> p (c b)").bitcast(I32))
+        w1_raw1 = second_space.tile([P, 4, H], F32, name="w1_raw1", offset=4 * T + 2 * N)
+        nc.sync.dma_start(w1_raw1[:], w1_rows(1))
         nc.vector.tensor_copy(
-            row_table[:].rearrange("p (a b) -> p a b", b=P), zeros[:].unsqueeze(1).to_broadcast([P, T // P, P])
+            row_table[0 : P - 2, :].rearrange("p (a b) -> p a b", b=P),
+            zeros[0 : P - 2, :].unsqueeze(1).to_broadcast([P - 2, T // P, P]),
         )
-        nc.sync.dma_start(row_table[0:1, :], gain[0:1, :])
-        nc.sync.dma_start(row_table[64:65, :], shift[0:1, :])
 
         x_table0 = first_space.tile([P, T], I32, name="x_table0", offset=0)
         nc.sync.dma_start(x_table0[:], x_words[0].rearrange("p c b -> p (c b)").bitcast(I32))
@@ -89,7 +95,7 @@ def tile_picked_zdq_mlprelu_po_kernel(
         nc.vector.tensor_copy(picked_scales[:], scale_table[:].indirect(offsets[:]))
         x_plane = keep.tile([P, S], U8, name="x_plane", align_bytes=64)
         nc.vector.tensor_copy(x_plane[:].bitcast(I32), picked_scales[:].bitcast(I32))
-        for o in reversed(range(PASSES)):
+        for o in range(PASSES):
             for r in range(1, 4):
                 nc.sync.dma_start(
                     x_plane[4 * o + r : P : 32, :].bitcast(I32), picked_scales[8 * r + 4 * o : P : 32, :].bitcast(I32)
@@ -102,9 +108,6 @@ def tile_picked_zdq_mlprelu_po_kernel(
 
         x_table1 = second_space.tile([P, T], I32, name="x_table1", offset=0)
         nc.sync.dma_start(x_table1[:], x_words[1].rearrange("p c b -> p (c b)").bitcast(I32))
-        w1_raw0 = second_space.tile([P, 2, 4, H // 2], F32, name="w1_raw0", offset=4 * T)
-        for half in range(2):
-            nc.sync.dma_start(w1_raw0[:, half], w1_rows(0)[:, :, H // 2 * half : H // 2 * (half + 1)])
 
         picked_rows = keep.tile([P, S], F32, name="picked_rows")
         nc.vector.tensor_copy(picked_rows[:], row_table[:].indirect(offsets[:]))
@@ -112,18 +115,31 @@ def tile_picked_zdq_mlprelu_po_kernel(
         x_code0 = keep.tile([P, S], U32, name="x_code0", align_bytes=64)
         nc.vector.tensor_copy(x_code0[:], x_table0[:].bitcast(U32).indirect(offsets[:]))
 
-        w2_plane = keep.tile([P, N], U8, name="w2_plane", align_bytes=64)
-        nc.gpsimd.tensor_copy(
+        w2_plane = first_space.tile([P, N], U8, name="w2_plane", align_bytes=64, offset=0)
+        nc.vector.tensor_copy(
             w2_plane[:].rearrange("p (t m) -> p t m", t=4), w2_raw_scales[:].rearrange("p (m t) -> p t m", t=4)
         )
 
-        factors = first_space.tile([P, TILES, 2], F32, name="factors", offset=4 * T)
+        w1_codes, w1_plane = [], []
+        for o, raw in enumerate([w1_raw0, w1_raw1]):
+            g = keep.tile([P, 4 * H], BF16, name="w1_grouped%d" % o, align_bytes=64)
+            nc.scalar.copy(
+                g[:].rearrange("p (u m e j) -> p u m j e", u=2, e=2, j=4),
+                raw[:].rearrange("p j (m u e) -> p u m j e", u=2, e=2),
+            )
+            codes = keep.tile([P, H], U32, name="w1_codes%d" % o, align_bytes=64)
+            plane = keep.tile([P, H], U8, name="w1_plane%d" % o, align_bytes=64)
+            nc.vector.quantize_mx(out=codes[:].bitcast(FP8X4), scales=plane[:], in_=g[:])
+            w1_codes.append(codes)
+            w1_plane.append(plane)
+
+        factors = second_space.tile([P, TILES, 2], F32, name="factors", offset=4 * T + 4 * N)
         for b in range(2):
             turned = bank(6 + b, [P, 4, P])
             for a in range(4):
                 jt = 4 * b + a
                 nc.tensor.transpose(turned[:, a, :], picked_rows[:, P * jt : P * (jt + 1)], ident[:])
-            nc.scalar.copy(factors[:, 4 * b : 4 * b + 4, :], turned[:, :, 0:P:64])
+            nc.scalar.copy(factors[:, 4 * b : 4 * b + 4, :], turned[:, :, P - 2 : P])
 
         offsets_term = []
         for jt in range(TILES):
@@ -136,34 +152,11 @@ def tile_picked_zdq_mlprelu_po_kernel(
             )
             offsets_term.append(term)
 
-        w1_codes = [keep.tile([P, H], U32, name="w1_codes%d" % o, align_bytes=64) for o in range(PASSES)]
-        w1_plane = [keep.tile([P, H], U8, name="w1_plane%d" % o, align_bytes=64) for o in range(PASSES)]
-        g = keep.tile([P, 4 * H], BF16, name="w1_grouped1", align_bytes=64)
-        nc.scalar.copy(
-            g[:].rearrange("p (u m e j) -> p u m j e", u=2, e=2, j=4),
-            w1_raw1[:].rearrange("p j (m u e) -> p u m j e", u=2, e=2),
-        )
-        nc.vector.quantize_mx(out=w1_codes[1][:].bitcast(FP8X4), scales=w1_plane[1][:], in_=g[:])
-
         x_code1 = [keep.tile([P, S // 2], U32, name="x_code1%d" % half, align_bytes=64) for half in range(2)]
         for half in range(2):
             nc.vector.tensor_copy(
                 x_code1[half][:], x_table1[:].bitcast(U32).indirect(offsets[:, S // 32 * half : S // 32 * (half + 1)])
             )
-
-        for half in range(2):
-            pieces = []
-            for u in range(2):
-                g = keep.tile([P, H], BF16, name="w1_grouped0%d%d" % (half, u), align_bytes=64)
-                copy = nc.vector.tensor_copy if (half, u) == (1, 1) else nc.scalar.copy
-                copy(
-                    g[:].rearrange("p (m e j) -> p m j e", e=2, j=4),
-                    w1_raw0[:, half].rearrange("p j (m u e) -> p u m j e", u=2, e=2)[:, u],
-                )
-                pieces.append(g)
-            for u in range(2):
-                cols = slice(H // 2 * u + H // 4 * half, H // 2 * u + H // 4 * (half + 1))
-                nc.vector.quantize_mx(out=w1_codes[0][:, cols].bitcast(FP8X4), scales=w1_plane[0][:, cols], in_=pieces[u][:])
 
         out_plane = keep.tile([P, S], U8, name="out_plane", align_bytes=64)
         out_codes = keep.tile([P, S], U32, name="out_codes", align_bytes=64)
@@ -195,9 +188,9 @@ def tile_picked_zdq_mlprelu_po_kernel(
 
         def first_layer(first, count):
             for jt in range(first, first + count):
-                product_pass(jt, 0)
                 if jt >= EARLY:
-                    product_pass(jt, 1)
+                    product_pass(jt, 0)
+                product_pass(jt, 1)
                 nc.vector.scalar_tensor_tensor(
                     out=pre[jt][:],
                     in0=sums[jt][:],
@@ -277,7 +270,7 @@ def tile_picked_zdq_mlprelu_po_kernel(
             (quantise_result, 5),
         ]
         for jt in range(EARLY):
-            product_pass(jt, 1)
+            product_pass(jt, 0)
         for step in range(len(chunks) + 5):
             for stage, lag in stages:
                 if 0 <= step - lag < len(chunks):

@@ -24,6 +24,7 @@ PASSES = K // 512
 TILES = S // P
 Y_BANKS = 6
 EARLY = 6
+SUMMED = 1
 
 
 def tile_picked_zdq_mlprelu_po_kernel(
@@ -144,12 +145,17 @@ def tile_picked_zdq_mlprelu_po_kernel(
         offsets_term = []
         for jt in range(TILES):
             term = keep.tile([P, H], F32, name="term%d" % jt)
-            nc.scalar.activation(
-                term[:].rearrange("p (u m e) -> p u m e", u=2, e=2),
-                wsum_rows[:].rearrange("p (u e) m -> p u m e", u=2),
-                COPY,
-                scale=factors[:, jt, 1:2],
-            )
+            if jt < SUMMED:
+                nc.scalar.activation(
+                    term[:], wsum_rows[:].rearrange("p t m -> p (t m)"), COPY, scale=factors[:, jt, 1:2]
+                )
+            else:
+                nc.scalar.activation(
+                    term[:].rearrange("p (u m e) -> p u m e", u=2, e=2),
+                    wsum_rows[:].rearrange("p (u e) m -> p u m e", u=2),
+                    COPY,
+                    scale=factors[:, jt, 1:2],
+                )
             offsets_term.append(term)
 
         x_code1 = [keep.tile([P, S // 2], U32, name="x_code1%d" % half, align_bytes=64) for half in range(2)]
@@ -164,10 +170,10 @@ def tile_picked_zdq_mlprelu_po_kernel(
         out_rows = out_0.rearrange("(p t) j -> p t j", t=4)
         out_words = out_1[0].rearrange("p c b -> p (c b)").bitcast(I32)
 
-        pre = [keep.tile([P, H], BF16, name="pre%d" % jt) for jt in range(TILES)]
+        pre = {jt: keep.tile([P, H], BF16, name="pre%d" % jt) for jt in range(SUMMED, TILES)}
         hidden, hidden_mx, result, rounded = {}, {}, {}, {}
 
-        sums = {}
+        sums, scaled = {}, {}
 
         def product_pass(jt, o):
             half, place = divmod(jt, TILES // 2)
@@ -191,6 +197,15 @@ def tile_picked_zdq_mlprelu_po_kernel(
                 if jt >= EARLY:
                     product_pass(jt, 0)
                 product_pass(jt, 1)
+                if jt < SUMMED:
+                    scaled[jt] = keep.tile([P, H], F32, name="scaled%d" % jt)
+                    nc.scalar.activation(
+                        scaled[jt][:].rearrange("p (u e m) -> p u e m", u=2, e=2),
+                        sums[jt][:].rearrange("p (u m e) -> p u e m", u=2, e=2),
+                        COPY,
+                        scale=factors[:, jt, 0:1],
+                    )
+                    continue
                 nc.vector.scalar_tensor_tensor(
                     out=pre[jt][:],
                     in0=sums[jt][:],
@@ -202,6 +217,24 @@ def tile_picked_zdq_mlprelu_po_kernel(
 
         def turn(first, count):
             n = P * count
+            if first < SUMMED:
+                turned = bank(6 + first % 2, [P, 4, P])
+                for t in range(4):
+                    for part, source in enumerate([offsets_term[first], scaled[first]]):
+                        nc.tensor.matmul(
+                            turned[:, t, :],
+                            source[:, P * t : P * (t + 1)],
+                            ident[:],
+                            start=part == 0,
+                            stop=part == 1,
+                            is_transpose=True,
+                        )
+                h = ring.tile([P, 4 * n], BF16, name="h", align_bytes=64)
+                nc.scalar.activation(
+                    h[:].rearrange("p (j t) -> p j t", t=4), turned[:].rearrange("p t j -> p j t"), RELU
+                )
+                hidden[first] = h
+                return
             turned = bank(6 + (first + 1) // 2 % 2, [P, 2, n])
             for a in range(count):
                 words = pre[first + a][:].bitcast(F32)
@@ -210,7 +243,7 @@ def tile_picked_zdq_mlprelu_po_kernel(
             h = ring.tile([P, 4 * n], BF16, name="h", align_bytes=64)
             pairs_out = h[:].rearrange("p (j u e) -> p j u e", u=2, e=2)
             pairs_in = turned[:].bitcast(BF16).rearrange("p u (j e) -> p j u e", e=2)
-            if first == 5:
+            if first >= 3:
                 nc.vector.tensor_scalar_max(pairs_out, pairs_in, 0.0)
             else:
                 nc.scalar.activation(pairs_out, pairs_in, RELU)
@@ -247,10 +280,21 @@ def tile_picked_zdq_mlprelu_po_kernel(
 
         def round_result(first, count):
             r = ring.tile([P, 4 * P * count], BF16, name="rounded", align_bytes=64)
-            nc.vector.tensor_copy(
-                r[:].rearrange("p (c i t) -> p c t i", i=4, t=4),
-                result[first][:].rearrange("p t (c i) -> p c t i", i=4),
-            )
+            if first < 3:
+                for a in range(count):
+                    nc.gpsimd.tensor_scalar(
+                        r[:, 4 * P * a : 4 * P * (a + 1)].rearrange("p (j t) -> p j t", t=4),
+                        result[first][:, :, P * a : P * (a + 1)].rearrange("p t j -> p j t"),
+                        1.0,
+                        -0.0,
+                        MULT,
+                        ADD,
+                    )
+            else:
+                nc.vector.tensor_copy(
+                    r[:].rearrange("p (c i t) -> p c t i", i=4, t=4),
+                    result[first][:].rearrange("p t (c i) -> p c t i", i=4),
+                )
             rounded[first] = r
 
         def quantise_result(first, count):

@@ -22,9 +22,8 @@ RELU = mybir.ActivationFunctionType.Relu
 P = 128
 PASSES = K // 512
 TILES = S // P
-Y_BANKS = 6
 EARLY = 6
-SUMMED = 1
+SUMMED = 2
 
 
 def tile_picked_zdq_mlprelu_po_kernel(
@@ -56,7 +55,7 @@ def tile_picked_zdq_mlprelu_po_kernel(
         w1_raw0 = keep.tile([P, 4, H], F32, name="w1_raw0")
         nc.sync.dma_start(w1_raw0[:], w1_rows(0))
 
-        first_zeros = second_space.tile([P, P], F32, name="first_zeros", offset=4 * T + 2 * N - 2 * P)
+        first_zeros = second_space.tile([P, P], F32, name="first_zeros", offset=4 * T + 4 * N)
         nc.vector.memset(first_zeros[:], 0.0)
 
         scale_table = scale_space.tile([P, T], U8, name="scale_table", offset=0)
@@ -73,9 +72,7 @@ def tile_picked_zdq_mlprelu_po_kernel(
 
         zeros = first_space.tile([P, P], F32, name="zeros", offset=4 * T - 4 * P)
         nc.vector.tensor_copy(zeros[:], first_zeros[:])
-        w2_raw = second_space.tile([P, N], I32, name="w2_raw", offset=4 * T - 2 * N)
-        nc.sync.dma_start(w2_raw[:], w2_words[0].rearrange("p c b -> p (c b)").bitcast(I32))
-        w1_raw1 = second_space.tile([P, 4, H], F32, name="w1_raw1", offset=4 * T + 2 * N)
+        w1_raw1 = second_space.tile([P, 4, H], F32, name="w1_raw1", offset=4 * T + 4 * N)
         nc.sync.dma_start(w1_raw1[:], w1_rows(1))
         nc.vector.tensor_copy(
             row_table[0 : P - 2, :].rearrange("p (a b) -> p a b", b=P),
@@ -88,7 +85,7 @@ def tile_picked_zdq_mlprelu_po_kernel(
         def bank(b, shape):
             return psum.tile(shape, F32, name="bank%d" % b, tag="bank%d" % b)
 
-        wsum_rows = bank(5, [P, 4, P])
+        wsum_rows = bank(EARLY - 1, [P, 4, P])
         for t in range(4):
             nc.tensor.transpose(wsum_rows[:, t, :], wsum_cols[:, t : t + 1].to_broadcast([P, P]), ident[:])
 
@@ -102,16 +99,29 @@ def tile_picked_zdq_mlprelu_po_kernel(
                     x_plane[4 * o + r : P : 32, :].bitcast(I32), picked_scales[8 * r + 4 * o : P : 32, :].bitcast(I32)
                 )
 
-        w2_codes = scale_space.tile([P, N], I32, name="w2_codes", align_bytes=64, offset=0)
-        nc.vector.tensor_copy(
-            w2_codes[:].rearrange("p (t m) -> p t m", t=4), w2_raw[:].rearrange("p (m t) -> p t m", t=4)
-        )
+        picked_rows = keep.tile([P, S], F32, name="picked_rows")
+        nc.vector.tensor_copy(picked_rows[:], row_table[:].indirect(offsets[:]))
+
+        grouped = [
+            second_space.tile([P, 4 * H], BF16, name="w1_grouped0", align_bytes=64, offset=4 * T - 4 * N),
+            keep.tile([P, 4 * H], BF16, name="w1_grouped1", align_bytes=64),
+        ]
+        w1_codes = [
+            scale_space.tile([P, H], U32, name="w1_codes0", align_bytes=64, offset=0),
+            keep.tile([P, H], U32, name="w1_codes1", align_bytes=64),
+        ]
+        w1_plane = [keep.tile([P, H], U8, name="w1_plane%d" % o, align_bytes=64) for o in range(PASSES)]
+        for o, raw in enumerate([w1_raw0, w1_raw1]):
+            nc.scalar.copy(
+                grouped[o][:].rearrange("p (u m e j) -> p u m j e", u=2, e=2, j=4),
+                raw[:].rearrange("p j (m u e) -> p u m j e", u=2, e=2),
+            )
+            nc.vector.quantize_mx(out=w1_codes[o][:].bitcast(FP8X4), scales=w1_plane[o][:], in_=grouped[o][:])
 
         x_table1 = second_space.tile([P, T], I32, name="x_table1", offset=0)
         nc.sync.dma_start(x_table1[:], x_words[1].rearrange("p c b -> p (c b)").bitcast(I32))
-
-        picked_rows = keep.tile([P, S], F32, name="picked_rows")
-        nc.vector.tensor_copy(picked_rows[:], row_table[:].indirect(offsets[:]))
+        w2_raw = second_space.tile([P, N], I32, name="w2_raw", offset=4 * T)
+        nc.sync.dma_start(w2_raw[:], w2_words[0].rearrange("p c b -> p (c b)").bitcast(I32))
 
         x_code0 = keep.tile([P, S], U32, name="x_code0", align_bytes=64)
         nc.vector.tensor_copy(x_code0[:], x_table0[:].bitcast(U32).indirect(offsets[:]))
@@ -121,34 +131,31 @@ def tile_picked_zdq_mlprelu_po_kernel(
             w2_plane[:].rearrange("p (t m) -> p t m", t=4), w2_raw_scales[:].rearrange("p (m t) -> p t m", t=4)
         )
 
-        w1_codes, w1_plane = [], []
-        for o, raw in enumerate([w1_raw0, w1_raw1]):
-            g = keep.tile([P, 4 * H], BF16, name="w1_grouped%d" % o, align_bytes=64)
-            nc.scalar.copy(
-                g[:].rearrange("p (u m e j) -> p u m j e", u=2, e=2, j=4),
-                raw[:].rearrange("p j (m u e) -> p u m j e", u=2, e=2),
-            )
-            codes = keep.tile([P, H], U32, name="w1_codes%d" % o, align_bytes=64)
-            plane = keep.tile([P, H], U8, name="w1_plane%d" % o, align_bytes=64)
-            nc.vector.quantize_mx(out=codes[:].bitcast(FP8X4), scales=plane[:], in_=g[:])
-            w1_codes.append(codes)
-            w1_plane.append(plane)
-
-        factors = second_space.tile([P, TILES, 2], F32, name="factors", offset=4 * T + 4 * N)
+        factors = second_space.tile([P, TILES, 2], F32, name="factors", offset=4 * T + 8 * N)
         for b in range(2):
-            turned = bank(6 + b, [P, 4, P])
+            turned = bank(EARLY - 3 + b, [P, 4, P])
             for a in range(4):
                 jt = 4 * b + a
                 nc.tensor.transpose(turned[:, a, :], picked_rows[:, P * jt : P * (jt + 1)], ident[:])
             nc.scalar.copy(factors[:, 4 * b : 4 * b + 4, :], turned[:, :, P - 2 : P])
 
-        offsets_term = []
+        offsets_term, turned_sum = [], {}
         for jt in range(TILES):
             term = keep.tile([P, H], F32, name="term%d" % jt)
             if jt < SUMMED:
                 nc.scalar.activation(
                     term[:], wsum_rows[:].rearrange("p t m -> p (t m)"), COPY, scale=factors[:, jt, 1:2]
                 )
+                turned_sum[jt] = (EARLY + jt, bank(EARLY + jt, [P, 4, P]))
+                for t in range(4):
+                    nc.tensor.matmul(
+                        turned_sum[jt][1][:, t, :],
+                        term[:, P * t : P * (t + 1)],
+                        ident[:],
+                        start=t == 0,
+                        stop=False,
+                        is_transpose=True,
+                    )
             else:
                 nc.scalar.activation(
                     term[:].rearrange("p (u m e) -> p u m e", u=2, e=2),
@@ -164,161 +171,235 @@ def tile_picked_zdq_mlprelu_po_kernel(
                 x_code1[half][:], x_table1[:].bitcast(U32).indirect(offsets[:, S // 32 * half : S // 32 * (half + 1)])
             )
 
+        w2_codes = keep.tile([P, N], I32, name="w2_codes", align_bytes=64)
+        nc.gpsimd.tensor_copy(
+            w2_codes[:].rearrange("p (t m) -> p t m", t=4), w2_raw[:].rearrange("p (m t) -> p t m", t=4)
+        )
+
         out_plane = keep.tile([P, S], U8, name="out_plane", align_bytes=64)
         out_codes = keep.tile([P, S], U32, name="out_codes", align_bytes=64)
-        word_stores = {1: 0, 5: 3, 7: 7}
         out_rows = out_0.rearrange("(p t) j -> p t j", t=4)
         out_words = out_1[0].rearrange("p c b -> p (c b)").bitcast(I32)
 
-        pre = {jt: keep.tile([P, H], BF16, name="pre%d" % jt) for jt in range(SUMMED, TILES)}
-        hidden, hidden_mx, result, rounded = {}, {}, {}, {}
-
-        sums, scaled = {}, {}
+        emptied = []
+        products = {}
+        sums, pre, turned_pairs, hidden, hidden_mx, result = {}, {}, {}, {}, {}, {}
+        rounded = keep.tile([P, 4 * S], BF16, name="rounded", align_bytes=64)
 
         def product_pass(jt, o):
             half, place = divmod(jt, TILES // 2)
             cols = slice(P * jt, P * (jt + 1))
-            opens = jt not in sums
-            if opens:
-                sums[jt] = bank(jt % Y_BANKS, [P, H])
+            if o == 0:
+                b = jt if jt < EARLY else emptied.pop(0)
+                sums[jt] = (b, bank(b, [P, H]))
             codes = x_code0[:, cols] if o == 0 else x_code1[half][:, P * place : P * (place + 1)]
             nc.tensor.matmul_mx(
-                out=sums[jt][:],
+                out=sums[jt][1][:],
                 lhsT=codes.bitcast(FP8X4),
                 lhsT_scale=x_plane[4 * o : P, cols],
                 rhs=w1_codes[o][:].bitcast(FP8X4),
                 rhs_scale=w1_plane[o][:],
-                start=opens,
-                stop=not opens,
+                start=o == 0,
+                stop=o == 1,
             )
 
-        def first_layer(first, count):
-            for jt in range(first, first + count):
-                if jt >= EARLY:
-                    product_pass(jt, 0)
-                product_pass(jt, 1)
-                if jt < SUMMED:
-                    scaled[jt] = keep.tile([P, H], F32, name="scaled%d" % jt)
-                    nc.scalar.activation(
-                        scaled[jt][:].rearrange("p (u e m) -> p u e m", u=2, e=2),
-                        sums[jt][:].rearrange("p (u m e) -> p u e m", u=2, e=2),
-                        COPY,
-                        scale=factors[:, jt, 0:1],
-                    )
-                    continue
-                nc.vector.scalar_tensor_tensor(
-                    out=pre[jt][:],
-                    in0=sums[jt][:],
-                    scalar=factors[:, jt, 0:1],
-                    in1=offsets_term[jt][:],
-                    op0=MULT,
-                    op1=ADD,
+        def close(jt):
+            if jt >= EARLY:
+                product_pass(jt, 0)
+            product_pass(jt, 1)
+
+        def combine(jt):
+            b, y = sums[jt]
+            if jt < SUMMED:
+                pre[jt] = keep.tile([P, H], F32, name="scaled%d" % jt)
+                nc.scalar.activation(
+                    pre[jt][:].rearrange("p (u e m) -> p u e m", u=2, e=2),
+                    y[:].rearrange("p (u m e) -> p u e m", u=2, e=2),
+                    COPY,
+                    scale=factors[:, jt, 0:1],
                 )
+            else:
+                pre[jt] = keep.tile([P, H], BF16, name="pre%d" % jt)
+                nc.vector.scalar_tensor_tensor(
+                    out=pre[jt][:], in0=y[:], scalar=factors[:, jt, 0:1], in1=offsets_term[jt][:], op0=MULT, op1=ADD
+                )
+            emptied.append(b)
 
         def turn(first, count):
-            n = P * count
             if first < SUMMED:
-                turned = bank(6 + first % 2, [P, 4, P])
                 for t in range(4):
-                    for part, source in enumerate([offsets_term[first], scaled[first]]):
-                        nc.tensor.matmul(
-                            turned[:, t, :],
-                            source[:, P * t : P * (t + 1)],
-                            ident[:],
-                            start=part == 0,
-                            stop=part == 1,
-                            is_transpose=True,
-                        )
-                h = ring.tile([P, 4 * n], BF16, name="h", align_bytes=64)
-                nc.scalar.activation(
-                    h[:].rearrange("p (j t) -> p j t", t=4), turned[:].rearrange("p t j -> p j t"), RELU
-                )
-                hidden[first] = h
+                    nc.tensor.matmul(
+                        turned_sum[first][1][:, t, :],
+                        pre[first][:, P * t : P * (t + 1)],
+                        ident[:],
+                        start=False,
+                        stop=t == 3,
+                        is_transpose=True,
+                    )
                 return
-            turned = bank(6 + (first + 1) // 2 % 2, [P, 2, n])
+            b = emptied.pop(0)
+            turned = bank(b, [P, 2, P * count])
             for a in range(count):
                 words = pre[first + a][:].bitcast(F32)
                 for u in range(2):
                     nc.tensor.transpose(turned[:, u, P * a : P * (a + 1)], words[:, P * u : P * (u + 1)], ident[:])
-            h = ring.tile([P, 4 * n], BF16, name="h", align_bytes=64)
-            pairs_out = h[:].rearrange("p (j u e) -> p j u e", u=2, e=2)
-            pairs_in = turned[:].bitcast(BF16).rearrange("p u (j e) -> p j u e", e=2)
-            if first >= 3:
-                nc.vector.tensor_scalar_max(pairs_out, pairs_in, 0.0)
+            turned_pairs[first] = (b, turned)
+
+        def rectify(first, count, on_vector):
+            h = keep.tile([P, 4 * P * count], BF16, name="h%d" % first, align_bytes=64)
+            if first < SUMMED:
+                b, turned = turned_sum[first]
+                nc.scalar.activation(
+                    h[:].rearrange("p (j t) -> p j t", t=4), turned[:].rearrange("p t j -> p j t"), RELU
+                )
             else:
-                nc.scalar.activation(pairs_out, pairs_in, RELU)
+                b, turned = turned_pairs[first]
+                pairs_out = h[:].rearrange("p (j u e) -> p j u e", u=2, e=2)
+                pairs_in = turned[:].bitcast(BF16).rearrange("p u (j e) -> p j u e", e=2)
+                if on_vector:
+                    nc.vector.tensor_scalar_max(pairs_out, pairs_in, 0.0)
+                else:
+                    nc.scalar.activation(pairs_out, pairs_in, RELU)
+            emptied.append(b)
             hidden[first] = h
 
         def quantise_hidden(first, count):
             n = P * count
-            codes = ring.tile([P, n], U32, name="h_codes", align_bytes=64)
-            plane = ring.tile([P, n], U8, name="h_plane", align_bytes=64)
+            codes = keep.tile([P, n], U32, name="h_codes%d" % first, align_bytes=64)
+            plane = keep.tile([P, n], U8, name="h_plane%d" % first, align_bytes=64)
             nc.vector.quantize_mx(out=codes[:].bitcast(FP8X4), scales=plane[:], in_=hidden[first][:])
             hidden_mx[first] = (codes, plane)
 
         def second_layer(first, count):
-            n = P * count
             codes, plane = hidden_mx[first]
-            res = keep.tile([P, 4, n], F32, name="res%d" % first)
-            per_bank = 4 // count
-            for part in range(count):
-                acc = bank((2 + first + part) % Y_BANKS, [P, per_bank, n])
-                for s in range(per_bank):
-                    t = per_bank * part + s
+            res = keep.tile([P, 4, P * count], F32, name="res%d" % first)
+            for a in range(count):
+                b = emptied.pop(0)
+                acc = bank(b, [P, 4, P])
+                for t in range(4):
                     nc.tensor.matmul_mx(
-                        out=acc[:, s, :],
+                        out=acc[:, t, :],
                         lhsT=w2_codes[:, P * t : P * (t + 1)].bitcast(FP8X4),
                         lhsT_scale=w2_plane[:, P * t : P * (t + 1)],
-                        rhs=codes[:].bitcast(FP8X4),
-                        rhs_scale=plane[:],
+                        rhs=codes[:, P * a : P * (a + 1)].bitcast(FP8X4),
+                        rhs_scale=plane[:, P * a : P * (a + 1)],
                         start=True,
                         stop=True,
                     )
-                nc.scalar.copy(res[:, per_bank * part : per_bank * (part + 1), :], acc[:])
-            nc.sync.dma_start(out_rows[:, :, P * first : P * first + n], res[:])
-            result[first] = res
+                products[first + a] = (b, acc)
+                result[first + a] = (res, a)
 
-        def round_result(first, count):
-            r = ring.tile([P, 4 * P * count], BF16, name="rounded", align_bytes=64)
-            if first < 3:
-                for a in range(count):
-                    nc.gpsimd.tensor_scalar(
-                        r[:, 4 * P * a : 4 * P * (a + 1)].rearrange("p (j t) -> p j t", t=4),
-                        result[first][:, :, P * a : P * (a + 1)].rearrange("p t j -> p j t"),
-                        1.0,
-                        -0.0,
-                        MULT,
-                        ADD,
-                    )
-            else:
-                nc.vector.tensor_copy(
-                    r[:].rearrange("p (c i t) -> p c t i", i=4, t=4),
-                    result[first][:].rearrange("p t (c i) -> p c t i", i=4),
+        def empty(jt, engine="s", last_reader=True):
+            b, acc = products[jt]
+            res, a = result[jt]
+            copy = nc.scalar.copy if engine == "s" else nc.vector.tensor_copy
+            copy(res[:, :, P * a : P * (a + 1)], acc[:])
+            if last_reader:
+                emptied.append(b)
+
+        def store(first, count):
+            res, a = result[first]
+            nc.sync.dma_start(out_rows[:, :, P * first : P * (first + count)], res[:, :, P * a : P * (a + count)])
+
+        def round_bank(jt, engine):
+            b, acc = products[jt]
+            copy = nc.scalar.copy if engine == "s" else nc.vector.tensor_copy
+            copy(rounded[:, 4 * P * jt : 4 * P * (jt + 1)].rearrange("p (j t) -> p j t", t=4), acc[:].rearrange("p t j -> p j t"))
+            emptied.append(b)
+
+        def round_result(first, count, engine):
+            res, a = result[first]
+            target = rounded[:, 4 * P * first : 4 * P * (first + count)]
+            source = res[:, :, P * a : P * (a + count)]
+            if engine == "g":
+                nc.gpsimd.tensor_scalar(
+                    target.rearrange("p (j t) -> p j t", t=4), source.rearrange("p t j -> p j t"), 1.0, -0.0, MULT, ADD
                 )
-            rounded[first] = r
+            else:
+                copy = nc.scalar.copy if engine == "s" else nc.vector.tensor_copy
+                copy(target.rearrange("p (c i t) -> p c t i", i=4, t=4), source.rearrange("p t (c i) -> p c t i", i=4))
 
         def quantise_result(first, count):
             cols = slice(P * first, P * (first + count))
-            nc.vector.quantize_mx(out=out_codes[:, cols].bitcast(FP8X4), scales=out_plane[:, cols], in_=rounded[first][:])
-            if first in word_stores:
-                done = slice(P * word_stores[first], P * (first + count))
-                nc.sync.dma_start(out_words[:, done], out_codes[:, done].bitcast(I32))
+            nc.vector.quantize_mx(
+                out=out_codes[:, cols].bitcast(FP8X4),
+                scales=out_plane[:, cols],
+                in_=rounded[:, 4 * P * first : 4 * P * (first + count)],
+            )
 
-        chunks = [(0, 1), (1, 2), (3, 2), (5, 2), (7, 1)]
-        stages = [
-            (first_layer, 0),
-            (turn, 1),
-            (quantise_hidden, 2),
-            (second_layer, 2),
-            (round_result, 4),
-            (quantise_result, 5),
-        ]
+        def store_words(first, last):
+            done = slice(P * first, P * last)
+            nc.sync.dma_start(out_words[:, done], out_codes[:, done].bitcast(I32))
+
         for jt in range(EARLY):
             product_pass(jt, 0)
-        for step in range(len(chunks) + 5):
-            for stage, lag in stages:
-                if 0 <= step - lag < len(chunks):
-                    stage(*chunks[step - lag])
+        close(0)
+        close(1)
+        close(2)
+        close(3)
+        combine(0)
+        combine(1)
+        close(4)
+        close(5)
+        combine(2)
+        combine(3)
+        turn(0, 1)
+        rectify(0, 1, False)
+        turn(1, 1)
+        turn(2, 2)
+        rectify(1, 1, False)
+        combine(4)
+        close(6)
+        quantise_hidden(0, 1)
+        second_layer(0, 1)
+        rectify(2, 2, True)
+        close(7)
+        quantise_hidden(1, 1)
+        second_layer(1, 1)
+        empty(0, "s", False)
+        store(0, 1)
+        combine(5)
+        turn(4, 2)
+        quantise_hidden(2, 2)
+        round_bank(0, "s")
+        empty(1, "s", False)
+        store(1, 1)
+        second_layer(2, 2)
+        combine(6)
+        combine(7)
+        turn(6, 2)
+        empty(2, "s", False)
+        store(2, 1)
+        empty(3)
+        store(3, 1)
+        rectify(4, 2, True)
+        round_bank(1, "s")
+        round_bank(2, "s")
+        quantise_result(0, 1)
+        quantise_hidden(4, 2)
+        second_layer(4, 2)
+        rectify(6, 2, True)
+        round_result(3, 1, "v")
+        quantise_hidden(6, 2)
+        second_layer(6, 2)
+        empty(4)
+        store(4, 1)
+        empty(5)
+        store(5, 1)
+        quantise_result(1, 1)
+        quantise_result(2, 2)
+        store_words(0, 4)
+        empty(6, "v")
+        store(6, 1)
+        round_result(4, 2, "v")
+        empty(7, "s", False)
+        store(7, 1)
+        round_bank(7, "s")
+        round_result(6, 1, "v")
+        quantise_result(4, 2)
+        store_words(4, 6)
+        quantise_result(6, 2)
+        store_words(6, 8)
 
         for q in range(4):
             queue = nc.sync if q % 2 == 0 else nc.scalar

@@ -41,10 +41,8 @@ def tile_picked_zdq_mlprelu_po_kernel(
         offsets = keep.tile([P, S // 16], U16, name="offsets")
         nc.sync.dma_start(offsets[:], offs)
 
-        ident = keep.tile([P, P], F32, name="ident")
-        make_identity(nc, ident[:])
         row_table = keep.tile([P, T], F32, name="row_table")
-        nc.sync.dma_start(row_table[P - 2 : P - 1, :], gain[0:1, :])
+        nc.sync.dma_start(row_table[P // 2 - 1 : P // 2, :], gain[0:1, :])
         nc.sync.dma_start(row_table[P - 1 : P, :], shift[0:1, :])
         wsum_cols = keep.tile([P, 4], F32, name="wsum_cols")
         nc.scalar.dma_start(wsum_cols[:], wsum.rearrange("(p t) o -> p (t o)", t=4))
@@ -55,7 +53,7 @@ def tile_picked_zdq_mlprelu_po_kernel(
         w1_raw0 = keep.tile([P, 4, H], F32, name="w1_raw0")
         nc.sync.dma_start(w1_raw0[:], w1_rows(0))
 
-        first_zeros = second_space.tile([P, P], F32, name="first_zeros", offset=4 * T + 4 * N)
+        first_zeros = second_space.tile([P, P], F32, name="first_zeros", offset=4 * T + 4 * N + 4 * S + 16 * H - 2 * P)
         nc.vector.memset(first_zeros[:], 0.0)
 
         scale_table = scale_space.tile([P, T], U8, name="scale_table", offset=0)
@@ -63,24 +61,23 @@ def tile_picked_zdq_mlprelu_po_kernel(
         for o in range(PASSES):
             nc.sync.dma_start(scale_table[4 * o : P : 8, :].bitcast(I32), x_scales[o].bitcast(I32))
 
-        w2_raw_scales = keep.tile([P, N], U8, name="w2_raw_scales")
-        nc.gpsimd.memset(w2_raw_scales[:].bitcast(I32), 0)
-        for q in range(4):
-            nc.gpsimd.dma_start(
-                w2_raw_scales[32 * q : 32 * q + 4, :].bitcast(I32), w2_scales[0, 4 * q : 4 * q + 4, :].bitcast(I32)
-            )
-
-        zeros = first_space.tile([P, P], F32, name="zeros", offset=4 * T - 4 * P)
+        zeros = first_space.tile([P, P], F32, name="zeros", offset=2 * P)
         nc.vector.tensor_copy(zeros[:], first_zeros[:])
-        w1_raw1 = second_space.tile([P, 4, H], F32, name="w1_raw1", offset=4 * T + 4 * N)
+        w1_raw1 = second_space.tile([P, 4, H], F32, name="w1_raw1", offset=4 * T + 4 * N + 4 * S)
         nc.sync.dma_start(w1_raw1[:], w1_rows(1))
-        nc.vector.tensor_copy(
-            row_table[0 : P - 2, :].rearrange("p (a b) -> p a b", b=P),
-            zeros[0 : P - 2, :].unsqueeze(1).to_broadcast([P - 2, T // P, P]),
-        )
-
-        x_table0 = first_space.tile([P, T], I32, name="x_table0", offset=0)
+        x_table0 = second_space.tile([P, T], I32, name="x_table0", offset=4 * T + 4 * N + 4 * S + 16 * H)
         nc.sync.dma_start(x_table0[:], x_words[0].rearrange("p c b -> p (c b)").bitcast(I32))
+
+        def fill(copy, rows, cols):
+            shape = [rows.stop - rows.start, (cols.stop - cols.start) // P, P]
+            copy(row_table[rows, cols].rearrange("p (a b) -> p a b", b=P), zeros[rows, :].unsqueeze(1).to_broadcast(shape))
+
+        fill(nc.scalar.copy, slice(P // 2, P - 1), slice(0, T // 2))
+        fill(nc.vector.tensor_copy, slice(0, P // 2 - 1), slice(0, T))
+        fill(nc.vector.tensor_copy, slice(P // 2, P - 1), slice(T // 2, T))
+
+        ident = first_space.tile([P, P], F32, name="ident", offset=0)
+        make_identity(nc, ident[:])
 
         def bank(b, shape):
             return psum.tile(shape, F32, name="bank%d" % b, tag="bank%d" % b)
@@ -99,11 +96,8 @@ def tile_picked_zdq_mlprelu_po_kernel(
                     x_plane[4 * o + r : P : 32, :].bitcast(I32), picked_scales[8 * r + 4 * o : P : 32, :].bitcast(I32)
                 )
 
-        picked_rows = keep.tile([P, S], F32, name="picked_rows")
-        nc.vector.tensor_copy(picked_rows[:], row_table[:].indirect(offsets[:]))
-
         grouped = [
-            second_space.tile([P, 4 * H], BF16, name="w1_grouped0", align_bytes=64, offset=4 * T - 4 * N),
+            second_space.tile([P, 4 * H], BF16, name="w1_grouped0", align_bytes=64, offset=4 * T - 2 * N),
             keep.tile([P, 4 * H], BF16, name="w1_grouped1", align_bytes=64),
         ]
         w1_codes = [
@@ -116,28 +110,38 @@ def tile_picked_zdq_mlprelu_po_kernel(
                 grouped[o][:].rearrange("p (u m e j) -> p u m j e", u=2, e=2, j=4),
                 raw[:].rearrange("p j (m u e) -> p u m j e", u=2, e=2),
             )
+
+        def quantise_w1(o):
             nc.vector.quantize_mx(out=w1_codes[o][:].bitcast(FP8X4), scales=w1_plane[o][:], in_=grouped[o][:])
+
+        quantise_w1(0)
 
         x_table1 = second_space.tile([P, T], I32, name="x_table1", offset=0)
         nc.sync.dma_start(x_table1[:], x_words[1].rearrange("p c b -> p (c b)").bitcast(I32))
         w2_raw = second_space.tile([P, N], I32, name="w2_raw", offset=4 * T)
         nc.sync.dma_start(w2_raw[:], w2_words[0].rearrange("p c b -> p (c b)").bitcast(I32))
 
+        picked_rows = second_space.tile([P, S], F32, name="picked_rows", offset=4 * T + 4 * N)
+        nc.vector.tensor_copy(picked_rows[:], row_table[:].indirect(offsets[:]))
+
+        quantise_w1(1)
         x_code0 = keep.tile([P, S], U32, name="x_code0", align_bytes=64)
         nc.vector.tensor_copy(x_code0[:], x_table0[:].bitcast(U32).indirect(offsets[:]))
 
-        w2_plane = first_space.tile([P, N], U8, name="w2_plane", align_bytes=64, offset=0)
-        nc.vector.tensor_copy(
-            w2_plane[:].rearrange("p (t m) -> p t m", t=4), w2_raw_scales[:].rearrange("p (m t) -> p t m", t=4)
-        )
+        w2_raw_scales = second_space.tile([P, N], U8, name="w2_raw_scales", offset=4 * T + 4 * N + 4 * S + 20 * H)
+        nc.vector.memset(w2_raw_scales[:].bitcast(I32), 0)
+        for q in range(4):
+            nc.sync.dma_start(
+                w2_raw_scales[32 * q : 32 * q + 4, :].bitcast(I32), w2_scales[0, 4 * q : 4 * q + 4, :].bitcast(I32)
+            )
 
-        factors = second_space.tile([P, TILES, 2], F32, name="factors", offset=4 * T + 8 * N)
+        factors = second_space.tile([P, TILES, 2], F32, name="factors", offset=4 * T + 8 * N + 4 * S)
         for b in range(2):
             turned = bank(EARLY - 3 + b, [P, 4, P])
             for a in range(4):
                 jt = 4 * b + a
                 nc.tensor.transpose(turned[:, a, :], picked_rows[:, P * jt : P * (jt + 1)], ident[:])
-            nc.scalar.copy(factors[:, 4 * b : 4 * b + 4, :], turned[:, :, P - 2 : P])
+            nc.scalar.copy(factors[:, 4 * b : 4 * b + 4, :], turned[:, :, P // 2 - 1 : P : P // 2])
 
         offsets_term, turned_sum = [], {}
         for jt in range(TILES):
@@ -174,6 +178,10 @@ def tile_picked_zdq_mlprelu_po_kernel(
         w2_codes = keep.tile([P, N], I32, name="w2_codes", align_bytes=64)
         nc.gpsimd.tensor_copy(
             w2_codes[:].rearrange("p (t m) -> p t m", t=4), w2_raw[:].rearrange("p (m t) -> p t m", t=4)
+        )
+        w2_plane = keep.tile([P, N], U8, name="w2_plane", align_bytes=64)
+        nc.gpsimd.tensor_copy(
+            w2_plane[:].rearrange("p (t m) -> p t m", t=4), w2_raw_scales[:].rearrange("p (m t) -> p t m", t=4)
         )
 
         out_plane = keep.tile([P, S], U8, name="out_plane", align_bytes=64)

@@ -377,9 +377,8 @@ def tile_picked_zdq_mlprelu_po_kernel(
         combine(7)
         turn(6, 2)
         empty(2, "s", False)
-        store(2, 1)
         empty(3)
-        store(3, 1)
+        store(2, 2)
         rectify(4, 2, True)
         round_bank(1, "s")
         round_bank(2, "s")
@@ -391,17 +390,15 @@ def tile_picked_zdq_mlprelu_po_kernel(
         quantise_hidden(6, 2)
         second_layer(6, 2)
         empty(4)
-        store(4, 1)
         empty(5)
-        store(5, 1)
+        store(4, 2)
         quantise_result(1, 1)
         quantise_result(2, 2)
         store_words(0, 4)
         empty(6, "v")
-        store(6, 1)
         round_result(4, 2, "v")
         empty(7, "s", False)
-        store(7, 1)
+        store(6, 2)
         round_bank(7, "s")
         round_result(6, 1, "v")
         quantise_result(4, 2)

@@ -175,11 +175,11 @@ def tile_picked_zdq_mlprelu_po_kernel(
                 x_code1[half][:], x_table1[:].bitcast(U32).indirect(offsets[:, S // 32 * half : S // 32 * (half + 1)])
             )
 
-        w2_codes = keep.tile([P, N], I32, name="w2_codes", align_bytes=64)
+        w2_codes = second_space.tile([P, N], I32, name="w2_codes", align_bytes=64, offset=0)
         nc.gpsimd.tensor_copy(
             w2_codes[:].rearrange("p (t m) -> p t m", t=4), w2_raw[:].rearrange("p (m t) -> p t m", t=4)
         )
-        w2_plane = keep.tile([P, N], U8, name="w2_plane", align_bytes=64)
+        w2_plane = second_space.tile([P, N], U8, name="w2_plane", align_bytes=64, offset=4 * N)
         nc.gpsimd.tensor_copy(
             w2_plane[:].rearrange("p (t m) -> p t m", t=4), w2_raw_scales[:].rearrange("p (m t) -> p t m", t=4)
         )

@@ -38,20 +38,19 @@ def tile_picked_zdq_mlprelu_po_kernel(
         second_space = ctx.enter_context(tc.tile_pool(name="second_space", bufs=1))
         psum = ctx.enter_context(tc.psum_pool(name="psum", bufs=1))
 
+        def w1_rows(o):
+            return w1[512 * o : 512 * (o + 1), :].rearrange("(p j) c -> p j c", j=4)
+
         offsets = keep.tile([P, S // 16], U16, name="offsets")
+        w1_raw0 = keep.tile([P, 4, H], F32, name="w1_raw0")
+        nc.sync.dma_start(w1_raw0[:], w1_rows(0))
         nc.sync.dma_start(offsets[:], offs)
 
         row_table = keep.tile([P, T], F32, name="row_table")
         nc.sync.dma_start(row_table[P // 2 - 1 : P // 2, :], gain[0:1, :])
         nc.sync.dma_start(row_table[P - 1 : P, :], shift[0:1, :])
         wsum_cols = keep.tile([P, 4], F32, name="wsum_cols")
-        nc.scalar.dma_start(wsum_cols[:], wsum.rearrange("(p t) o -> p (t o)", t=4))
-
-        def w1_rows(o):
-            return w1[512 * o : 512 * (o + 1), :].rearrange("(p j) c -> p j c", j=4)
-
-        w1_raw0 = keep.tile([P, 4, H], F32, name="w1_raw0")
-        nc.sync.dma_start(w1_raw0[:], w1_rows(0))
+        nc.sync.dma_start(wsum_cols[:], wsum.rearrange("(p t) o -> p (t o)", t=4))
 
         first_zeros = second_space.tile([P, P], F32, name="first_zeros", offset=4 * T + 4 * N + 4 * S + 16 * H - 2 * P)
         nc.vector.memset(first_zeros[:], 0.0)
@@ -97,8 +96,8 @@ def tile_picked_zdq_mlprelu_po_kernel(
                 )
 
         grouped = [
-            second_space.tile([P, 4 * H], BF16, name="w1_grouped0", align_bytes=64, offset=4 * T - 2 * N),
-            keep.tile([P, 4 * H], BF16, name="w1_grouped1", align_bytes=64),
+            second_space.tile([P, 4 * H], BF16, name="w1_grouped0", align_bytes=64, offset=4 * T - 64),
+            second_space.tile([P, 4 * H], BF16, name="w1_grouped1", align_bytes=64, offset=8 * T + 4 * N + 4 * S + 16 * H),
         ]
         w1_codes = [
             scale_space.tile([P, H], U32, name="w1_codes0", align_bytes=64, offset=0),
@@ -118,13 +117,18 @@ def tile_picked_zdq_mlprelu_po_kernel(
 
         x_table1 = second_space.tile([P, T], I32, name="x_table1", offset=0)
         nc.sync.dma_start(x_table1[:], x_words[1].rearrange("p c b -> p (c b)").bitcast(I32))
-        w2_raw = second_space.tile([P, N], I32, name="w2_raw", offset=4 * T)
-        nc.sync.dma_start(w2_raw[:], w2_words[0].rearrange("p c b -> p (c b)").bitcast(I32))
 
-        picked_rows = second_space.tile([P, S], F32, name="picked_rows", offset=4 * T + 4 * N)
-        nc.vector.tensor_copy(picked_rows[:], row_table[:].indirect(offsets[:]))
+        picked_rows = [
+            second_space.tile([P, S // 2], F32, name="picked_rows%d" % half, offset=4 * T + 2 * S * half) for half in range(2)
+        ]
+        for half in range(2):
+            nc.vector.tensor_copy(
+                picked_rows[half][:], row_table[:].indirect(offsets[:, S // 32 * half : S // 32 * (half + 1)])
+            )
 
         quantise_w1(1)
+        w2_raw = second_space.tile([P, N], I32, name="w2_raw", offset=8 * T + 4 * N + 4 * S + 16 * H)
+        nc.sync.dma_start(w2_raw[:], w2_words[0].rearrange("p c b -> p (c b)").bitcast(I32))
         x_code0 = keep.tile([P, S], U32, name="x_code0", align_bytes=64)
         nc.vector.tensor_copy(x_code0[:], x_table0[:].bitcast(U32).indirect(offsets[:]))
 
@@ -136,15 +140,17 @@ def tile_picked_zdq_mlprelu_po_kernel(
             )
 
         factors = second_space.tile([P, TILES, 2], F32, name="factors", offset=4 * T + 8 * N + 4 * S)
-        for b in range(2):
-            turned = bank(EARLY - 3 + b, [P, 4, P])
+        def turn_factors(half):
+            turned = bank(EARLY - 2, [P, 4, P])
             for a in range(4):
-                jt = 4 * b + a
-                nc.tensor.transpose(turned[:, a, :], picked_rows[:, P * jt : P * (jt + 1)], ident[:])
-            nc.scalar.copy(factors[:, 4 * b : 4 * b + 4, :], turned[:, :, P // 2 - 1 : P : P // 2])
+                nc.tensor.transpose(turned[:, a, :], picked_rows[half][:, P * a : P * (a + 1)], ident[:])
+            nc.scalar.copy(factors[:, 4 * half : 4 * half + 4, :], turned[:, :, P // 2 - 1 : P : P // 2])
 
         offsets_term, turned_sum = [], {}
+        turn_factors(0)
         for jt in range(TILES):
+            if jt == SUMMED:
+                turn_factors(1)
             term = keep.tile([P, H], F32, name="term%d" % jt)
             if jt < SUMMED:
                 nc.scalar.activation(

@@ -20,10 +20,12 @@ COPY = mybir.ActivationFunctionType.Copy
 RELU = mybir.ActivationFunctionType.Relu
 
 P = 128
+BANKS = 8
 PASSES = K // 512
 TILES = S // P
-EARLY = 6
-SUMMED = 2
+SUMMED = [0, 1]
+EARLY = [0, 1, 2, 3, 4, 5]
+STORES = [(0, 1), (1, 1), (2, 2), (4, 2), (6, 2)]
 
 
 def tile_picked_zdq_mlprelu_po_kernel(
@@ -32,7 +34,7 @@ def tile_picked_zdq_mlprelu_po_kernel(
     nc = tc.nc
     with ExitStack() as ctx:
         keep = ctx.enter_context(tc.tile_pool(name="keep", bufs=1))
-        ring = ctx.enter_context(tc.tile_pool(name="ring", bufs=3))
+        stage = ctx.enter_context(tc.tile_pool(name="stage", bufs=1))
         first_space = ctx.enter_context(tc.tile_pool(name="first_space", bufs=1))
         scale_space = ctx.enter_context(tc.tile_pool(name="scale_space", bufs=1))
         second_space = ctx.enter_context(tc.tile_pool(name="second_space", bufs=1))
@@ -81,7 +83,7 @@ def tile_picked_zdq_mlprelu_po_kernel(
         def bank(b, shape):
             return psum.tile(shape, F32, name="bank%d" % b, tag="bank%d" % b)
 
-        wsum_rows = bank(EARLY - 1, [P, 4, P])
+        wsum_rows = bank(len(EARLY) - 1, [P, 4, P])
         for t in range(4):
             nc.tensor.transpose(wsum_rows[:, t, :], wsum_cols[:, t : t + 1].to_broadcast([P, P]), ident[:])
 
@@ -141,22 +143,23 @@ def tile_picked_zdq_mlprelu_po_kernel(
 
         factors = second_space.tile([P, TILES, 2], F32, name="factors", offset=4 * T + 8 * N + 4 * S)
         def turn_factors(half):
-            turned = bank(EARLY - 2, [P, 4, P])
+            turned = bank(len(EARLY) - 2, [P, 4, P])
             for a in range(4):
                 nc.tensor.transpose(turned[:, a, :], picked_rows[half][:, P * a : P * (a + 1)], ident[:])
             nc.scalar.copy(factors[:, 4 * half : 4 * half + 4, :], turned[:, :, P // 2 - 1 : P : P // 2])
 
-        offsets_term, turned_sum = [], {}
+        offsets_term, turned_sum = {}, {}
         turn_factors(0)
         for jt in range(TILES):
-            if jt == SUMMED:
+            if jt == len(SUMMED):
                 turn_factors(1)
             term = keep.tile([P, H], F32, name="term%d" % jt)
-            if jt < SUMMED:
+            if jt in SUMMED:
                 nc.scalar.activation(
                     term[:], wsum_rows[:].rearrange("p t m -> p (t m)"), COPY, scale=factors[:, jt, 1:2]
                 )
-                turned_sum[jt] = (EARLY + jt, bank(EARLY + jt, [P, 4, P]))
+                b = len(EARLY) + SUMMED.index(jt)
+                turned_sum[jt] = (b, bank(b, [P, 4, P]))
                 for t in range(4):
                     nc.tensor.matmul(
                         turned_sum[jt][1][:, t, :],
@@ -173,7 +176,7 @@ def tile_picked_zdq_mlprelu_po_kernel(
                     COPY,
                     scale=factors[:, jt, 1:2],
                 )
-            offsets_term.append(term)
+            offsets_term[jt] = term
 
         x_code1 = [keep.tile([P, S // 2], U32, name="x_code1%d" % half, align_bytes=64) for half in range(2)]
         for half in range(2):
@@ -190,41 +193,49 @@ def tile_picked_zdq_mlprelu_po_kernel(
             w2_plane[:].rearrange("p (t m) -> p t m", t=4), w2_raw_scales[:].rearrange("p (m t) -> p t m", t=4)
         )
 
+        def x_codes(jt, o):
+            half, place = divmod(jt, TILES // 2)
+            if o == 0:
+                return x_code0[:, P * jt : P * (jt + 1)]
+            return x_code1[half][:, P * place : P * (place + 1)]
+
         out_plane = keep.tile([P, S], U8, name="out_plane", align_bytes=64)
         out_codes = keep.tile([P, S], U32, name="out_codes", align_bytes=64)
         out_rows = out_0.rearrange("(p t) j -> p t j", t=4)
         out_words = out_1[0].rearrange("p c b -> p (c b)").bitcast(I32)
 
-        emptied = []
-        products = {}
-        sums, pre, turned_pairs, hidden, hidden_mx, result = {}, {}, {}, {}, {}, {}
-        rounded = keep.tile([P, 4 * S], BF16, name="rounded", align_bytes=64)
+        sums, pre, turned_pairs, products, result = {}, {}, {}, {}, {}
+        hidden_mx, rounded = {}, {}
+        hidden = keep.tile([P, 4 * S], BF16, name="hidden", align_bytes=64)
+        for first, count in STORES:
+            res = keep.tile([P, 4, P * count], F32, name="res%d" % first)
+            for a in range(count):
+                result[first + a] = (res, a)
 
-        def product_pass(jt, o):
-            half, place = divmod(jt, TILES // 2)
-            cols = slice(P * jt, P * (jt + 1))
+        def copier(engine):
+            return {"s": nc.scalar.copy, "v": nc.vector.tensor_copy}[engine]
+
+        def product_pass(jt, o, b=None):
             if o == 0:
-                b = jt if jt < EARLY else emptied.pop(0)
                 sums[jt] = (b, bank(b, [P, H]))
-            codes = x_code0[:, cols] if o == 0 else x_code1[half][:, P * place : P * (place + 1)]
             nc.tensor.matmul_mx(
                 out=sums[jt][1][:],
-                lhsT=codes.bitcast(FP8X4),
-                lhsT_scale=x_plane[4 * o : P, cols],
+                lhsT=x_codes(jt, o).bitcast(FP8X4),
+                lhsT_scale=x_plane[4 * o : P, P * jt : P * (jt + 1)],
                 rhs=w1_codes[o][:].bitcast(FP8X4),
                 rhs_scale=w1_plane[o][:],
                 start=o == 0,
                 stop=o == 1,
             )
 
-        def close(jt):
-            if jt >= EARLY:
-                product_pass(jt, 0)
+        def close(jt, b=None):
+            if jt not in EARLY:
+                product_pass(jt, 0, b)
             product_pass(jt, 1)
 
         def combine(jt):
             b, y = sums[jt]
-            if jt < SUMMED:
+            if jt in SUMMED:
                 pre[jt] = keep.tile([P, H], F32, name="scaled%d" % jt)
                 nc.scalar.activation(
                     pre[jt][:].rearrange("p (u e m) -> p u e m", u=2, e=2),
@@ -237,10 +248,9 @@ def tile_picked_zdq_mlprelu_po_kernel(
                 nc.vector.scalar_tensor_tensor(
                     out=pre[jt][:], in0=y[:], scalar=factors[:, jt, 0:1], in1=offsets_term[jt][:], op0=MULT, op1=ADD
                 )
-            emptied.append(b)
 
-        def turn(first, count):
-            if first < SUMMED:
+        def turn(first, count=1, b=None):
+            if first in SUMMED:
                 for t in range(4):
                     nc.tensor.matmul(
                         turned_sum[first][1][:, t, :],
@@ -251,7 +261,6 @@ def tile_picked_zdq_mlprelu_po_kernel(
                         is_transpose=True,
                     )
                 return
-            b = emptied.pop(0)
             turned = bank(b, [P, 2, P * count])
             for a in range(count):
                 words = pre[first + a][:].bitcast(F32)
@@ -259,94 +268,104 @@ def tile_picked_zdq_mlprelu_po_kernel(
                     nc.tensor.transpose(turned[:, u, P * a : P * (a + 1)], words[:, P * u : P * (u + 1)], ident[:])
             turned_pairs[first] = (b, turned)
 
-        def rectify(first, count, on_vector):
-            h = keep.tile([P, 4 * P * count], BF16, name="h%d" % first, align_bytes=64)
-            if first < SUMMED:
+        def rectify(first, count=1, engine="v"):
+            h = hidden[:, 4 * P * first : 4 * P * (first + count)]
+            if first in SUMMED:
                 b, turned = turned_sum[first]
-                nc.scalar.activation(
-                    h[:].rearrange("p (j t) -> p j t", t=4), turned[:].rearrange("p t j -> p j t"), RELU
-                )
+                target, source = h.rearrange("p (j t) -> p j t", t=4), turned[:].rearrange("p t j -> p j t")
             else:
                 b, turned = turned_pairs[first]
-                pairs_out = h[:].rearrange("p (j u e) -> p j u e", u=2, e=2)
-                pairs_in = turned[:].bitcast(BF16).rearrange("p u (j e) -> p j u e", e=2)
-                if on_vector:
-                    nc.vector.tensor_scalar_max(pairs_out, pairs_in, 0.0)
-                else:
-                    nc.scalar.activation(pairs_out, pairs_in, RELU)
-            emptied.append(b)
-            hidden[first] = h
+                target = h.rearrange("p (j u e) -> p j u e", u=2, e=2)
+                source = turned[:].bitcast(BF16).rearrange("p u (j e) -> p j u e", e=2)
+            if engine == "v":
+                nc.vector.tensor_scalar_max(target, source, 0.0)
+            else:
+                nc.scalar.activation(target, source, RELU)
 
-        def quantise_hidden(first, count):
-            n = P * count
-            codes = keep.tile([P, n], U32, name="h_codes%d" % first, align_bytes=64)
-            plane = keep.tile([P, n], U8, name="h_plane%d" % first, align_bytes=64)
-            nc.vector.quantize_mx(out=codes[:].bitcast(FP8X4), scales=plane[:], in_=hidden[first][:])
-            hidden_mx[first] = (codes, plane)
-
-        def second_layer(first, count):
-            codes, plane = hidden_mx[first]
-            res = keep.tile([P, 4, P * count], F32, name="res%d" % first)
+        def quantise_hidden(first, count=1):
+            codes = keep.tile([P, P * count], U32, name="h_codes%d" % first, align_bytes=64)
+            plane = keep.tile([P, P * count], U8, name="h_plane%d" % first, align_bytes=64)
+            nc.vector.quantize_mx(out=codes[:].bitcast(FP8X4), scales=plane[:], in_=hidden[:, 4 * P * first : 4 * P * (first + count)])
             for a in range(count):
-                b = emptied.pop(0)
+                hidden_mx[first + a] = (codes[:, P * a : P * (a + 1)], plane[:, P * a : P * (a + 1)])
+
+        def second_layer(first, *banks):
+            for jt, b in enumerate(banks, first):
+                codes, plane = hidden_mx[jt]
                 acc = bank(b, [P, 4, P])
                 for t in range(4):
                     nc.tensor.matmul_mx(
                         out=acc[:, t, :],
                         lhsT=w2_codes[:, P * t : P * (t + 1)].bitcast(FP8X4),
                         lhsT_scale=w2_plane[:, P * t : P * (t + 1)],
-                        rhs=codes[:, P * a : P * (a + 1)].bitcast(FP8X4),
-                        rhs_scale=plane[:, P * a : P * (a + 1)],
+                        rhs=codes.bitcast(FP8X4),
+                        rhs_scale=plane,
                         start=True,
                         stop=True,
                     )
-                products[first + a] = (b, acc)
-                result[first + a] = (res, a)
+                products[jt] = (b, acc)
 
-        def empty(jt, engine="s", last_reader=True):
+        def empty(jt, engine="s"):
             b, acc = products[jt]
             res, a = result[jt]
-            copy = nc.scalar.copy if engine == "s" else nc.vector.tensor_copy
-            copy(res[:, :, P * a : P * (a + 1)], acc[:])
-            if last_reader:
-                emptied.append(b)
+            copier(engine)(res[:, :, P * a : P * (a + 1)], acc[:])
 
-        def store(first, count):
+        def store(first):
             res, a = result[first]
-            nc.sync.dma_start(out_rows[:, :, P * first : P * (first + count)], res[:, :, P * a : P * (a + count)])
+            nc.sync.dma_start(out_rows[:, :, P * first : P * first + res[:].shape[2]], res[:])
 
-        def round_bank(jt, engine):
+        def rounded_tile(first, count, on=None):
+            if on is None:
+                tile = keep.tile([P, 4 * P * count], BF16, name="rounded%d" % first, align_bytes=64)
+            else:
+                tile = stage.tile([P, 4 * P * count], BF16, name="rounded%d" % first, align_bytes=64, offset=8 * P * on)
+            for a in range(count):
+                rounded[first + a] = (tile, a)
+
+        def rounded_cols(first, count):
+            tile, a = rounded[first]
+            return tile[:, 4 * P * a : 4 * P * (a + count)]
+
+        def round_bank(jt, engine="s"):
             b, acc = products[jt]
-            copy = nc.scalar.copy if engine == "s" else nc.vector.tensor_copy
-            copy(rounded[:, 4 * P * jt : 4 * P * (jt + 1)].rearrange("p (j t) -> p j t", t=4), acc[:].rearrange("p t j -> p j t"))
-            emptied.append(b)
+            copier(engine)(
+                rounded_cols(jt, 1).rearrange("p (j t) -> p j t", t=4),
+                acc[:].rearrange("p t j -> p j t"),
+            )
 
-        def round_result(first, count, engine):
+        def round_result(first, count=1, engine="v"):
             res, a = result[first]
-            target = rounded[:, 4 * P * first : 4 * P * (first + count)]
+            target = rounded_cols(first, count)
             source = res[:, :, P * a : P * (a + count)]
             if engine == "g":
                 nc.gpsimd.tensor_scalar(
-                    target.rearrange("p (j t) -> p j t", t=4), source.rearrange("p t j -> p j t"), 1.0, -0.0, MULT, ADD
+                    target.rearrange("p (j t) -> p j t", t=4),
+                    source.rearrange("p t j -> p j t"),
+                    1.0,
+                    -0.0,
+                    MULT,
+                    ADD,
                 )
             else:
-                copy = nc.scalar.copy if engine == "s" else nc.vector.tensor_copy
-                copy(target.rearrange("p (c i t) -> p c t i", i=4, t=4), source.rearrange("p t (c i) -> p c t i", i=4))
+                copier(engine)(
+                    target.rearrange("p (c i t) -> p c t i", i=4, t=4), source.rearrange("p t (c i) -> p c t i", i=4)
+                )
 
-        def quantise_result(first, count):
+        def quantise_result(first, count=1):
             cols = slice(P * first, P * (first + count))
             nc.vector.quantize_mx(
                 out=out_codes[:, cols].bitcast(FP8X4),
                 scales=out_plane[:, cols],
-                in_=rounded[:, 4 * P * first : 4 * P * (first + count)],
+                in_=rounded_cols(first, count),
             )
 
         def store_words(first, last):
             done = slice(P * first, P * last)
             nc.sync.dma_start(out_words[:, done], out_codes[:, done].bitcast(I32))
 
-        for jt in range(EARLY):
-            product_pass(jt, 0)
+        for b, jt in enumerate(EARLY):
+            product_pass(jt, 0, b)
+        rounded_tile(0, 8)
         close(0)
         close(1)
         close(2)
@@ -357,56 +376,58 @@ def tile_picked_zdq_mlprelu_po_kernel(
         close(5)
         combine(2)
         combine(3)
-        turn(0, 1)
-        rectify(0, 1, False)
-        turn(1, 1)
-        turn(2, 2)
-        rectify(1, 1, False)
+        turn(0)
+        rectify(0, 1, "s")
+        turn(1)
+        turn(2, 1, 0)
+        turn(3, 1, 1)
+        rectify(1, 1, "s")
+        rectify(2, 1, "s")
         combine(4)
-        close(6)
-        quantise_hidden(0, 1)
-        second_layer(0, 1)
-        rectify(2, 2, True)
-        close(7)
-        quantise_hidden(1, 1)
-        second_layer(1, 1)
-        empty(0, "s", False)
-        store(0, 1)
+        close(6, 2)
+        quantise_hidden(0)
+        second_layer(0, 3)
+        rectify(3, 1)
+        close(7, 4)
+        quantise_hidden(1)
+        second_layer(1, 6)
+        empty(0)
+        store(0)
         combine(5)
-        turn(4, 2)
+        turn(4, 2, 7)
         quantise_hidden(2, 2)
-        round_bank(0, "s")
-        empty(1, "s", False)
-        store(1, 1)
-        second_layer(2, 2)
+        round_bank(0)
+        empty(1)
+        store(1)
+        second_layer(2, 5, 1)
         combine(6)
         combine(7)
-        turn(6, 2)
-        empty(2, "s", False)
+        turn(6, 2, 0)
+        empty(2)
         empty(3)
-        store(2, 2)
-        rectify(4, 2, True)
-        round_bank(1, "s")
-        round_bank(2, "s")
-        quantise_result(0, 1)
+        store(2)
+        rectify(4, 2)
+        round_bank(1)
+        round_bank(2)
+        quantise_result(0)
         quantise_hidden(4, 2)
-        second_layer(4, 2)
-        rectify(6, 2, True)
-        round_result(3, 1, "v")
+        second_layer(4, 2, 3)
+        rectify(6, 2)
+        round_result(3)
         quantise_hidden(6, 2)
-        second_layer(6, 2)
+        second_layer(6, 4, 7)
         empty(4)
         empty(5)
-        store(4, 2)
-        quantise_result(1, 1)
+        store(4)
+        quantise_result(1)
         quantise_result(2, 2)
         store_words(0, 4)
         empty(6, "v")
-        round_result(4, 2, "v")
-        empty(7, "s", False)
-        store(6, 2)
-        round_bank(7, "s")
-        round_result(6, 1, "v")
+        round_result(4, 2)
+        empty(7)
+        store(6)
+        round_bank(7)
+        round_result(6)
         quantise_result(4, 2)
         store_words(4, 6)
         quantise_result(6, 2)

@@ -396,7 +396,7 @@ def tile_picked_zdq_mlprelu_po_kernel(
         combine(5)
         turn(4, 2, 7)
         quantise_hidden(2, 2)
-        round_bank(0)
+        round_result(0, 1, "g")
         empty(1)
         store(1)
         second_layer(2, 5, 1)
@@ -409,17 +409,16 @@ def tile_picked_zdq_mlprelu_po_kernel(
         rectify(4, 2)
         round_bank(1)
         round_bank(2)
-        quantise_result(0)
         quantise_hidden(4, 2)
         second_layer(4, 2, 3)
         rectify(6, 2)
-        round_result(3)
+        quantise_result(0, 2)
         quantise_hidden(6, 2)
         second_layer(6, 4, 7)
+        round_result(3)
         empty(4)
         empty(5)
         store(4)
-        quantise_result(1)
         quantise_result(2, 2)
         store_words(0, 4)
         empty(6, "v")

@@ -20,11 +20,12 @@ COPY = mybir.ActivationFunctionType.Copy
 RELU = mybir.ActivationFunctionType.Relu
 
 P = 128
-BANKS = 8
 PASSES = K // 512
 TILES = S // P
+RUN = T // P
 SUMMED = [0, 1]
 EARLY = [0, 1, 2, 3, 4, 5]
+CHUNKS = [(0, 1), (1, 1), (2, 2), (4, 2), (6, 2)]
 STORES = [(0, 1), (1, 1), (2, 2), (4, 2), (6, 2)]
 
 
@@ -34,56 +35,56 @@ def tile_picked_zdq_mlprelu_po_kernel(
     nc = tc.nc
     with ExitStack() as ctx:
         keep = ctx.enter_context(tc.tile_pool(name="keep", bufs=1))
-        stage = ctx.enter_context(tc.tile_pool(name="stage", bufs=1))
-        first_space = ctx.enter_context(tc.tile_pool(name="first_space", bufs=1))
         scale_space = ctx.enter_context(tc.tile_pool(name="scale_space", bufs=1))
-        second_space = ctx.enter_context(tc.tile_pool(name="second_space", bufs=1))
+        shared = ctx.enter_context(tc.tile_pool(name="shared", bufs=1))
         psum = ctx.enter_context(tc.psum_pool(name="psum", bufs=1))
-
-        def w1_rows(o):
-            return w1[512 * o : 512 * (o + 1), :].rearrange("(p j) c -> p j c", j=4)
-
-        offsets = keep.tile([P, S // 16], U16, name="offsets")
-        w1_raw0 = keep.tile([P, 4, H], F32, name="w1_raw0")
-        nc.sync.dma_start(w1_raw0[:], w1_rows(0))
-        nc.sync.dma_start(offsets[:], offs)
-
-        row_table = keep.tile([P, T], F32, name="row_table")
-        nc.sync.dma_start(row_table[P // 2 - 1 : P // 2, :], gain[0:1, :])
-        nc.sync.dma_start(row_table[P - 1 : P, :], shift[0:1, :])
-        wsum_cols = keep.tile([P, 4], F32, name="wsum_cols")
-        nc.sync.dma_start(wsum_cols[:], wsum.rearrange("(p t) o -> p (t o)", t=4))
-
-        first_zeros = second_space.tile([P, P], F32, name="first_zeros", offset=4 * T + 4 * N + 4 * S + 16 * H - 2 * P)
-        nc.vector.memset(first_zeros[:], 0.0)
-
-        scale_table = scale_space.tile([P, T], U8, name="scale_table", offset=0)
-        nc.vector.memset(scale_table[:].bitcast(I32), 0)
-        for o in range(PASSES):
-            nc.sync.dma_start(scale_table[4 * o : P : 8, :].bitcast(I32), x_scales[o].bitcast(I32))
-
-        zeros = first_space.tile([P, P], F32, name="zeros", offset=2 * P)
-        nc.vector.tensor_copy(zeros[:], first_zeros[:])
-        w1_raw1 = second_space.tile([P, 4, H], F32, name="w1_raw1", offset=4 * T + 4 * N + 4 * S)
-        nc.sync.dma_start(w1_raw1[:], w1_rows(1))
-        x_table0 = second_space.tile([P, T], I32, name="x_table0", offset=4 * T + 4 * N + 4 * S + 16 * H)
-        nc.sync.dma_start(x_table0[:], x_words[0].rearrange("p c b -> p (c b)").bitcast(I32))
-
-        def fill(copy, rows, cols):
-            shape = [rows.stop - rows.start, (cols.stop - cols.start) // P, P]
-            copy(row_table[rows, cols].rearrange("p (a b) -> p a b", b=P), zeros[rows, :].unsqueeze(1).to_broadcast(shape))
-
-        fill(nc.scalar.copy, slice(P // 2, P - 1), slice(0, T // 2))
-        fill(nc.vector.tensor_copy, slice(0, P // 2 - 1), slice(0, T))
-        fill(nc.vector.tensor_copy, slice(P // 2, P - 1), slice(T // 2, T))
-
-        ident = first_space.tile([P, P], F32, name="ident", offset=0)
-        make_identity(nc, ident[:])
 
         def bank(b, shape):
             return psum.tile(shape, F32, name="bank%d" % b, tag="bank%d" % b)
 
-        wsum_rows = bank(len(EARLY) - 1, [P, 4, P])
+        def copier(engine):
+            return {"s": nc.scalar.copy, "v": nc.vector.tensor_copy}[engine]
+
+        def w1_rows(o):
+            return w1[512 * o : 512 * (o + 1), :].rearrange("(p j) c -> p j c", j=4)
+
+        runs = keep.tile([P, RUN + P], F32, name="runs")
+        nc.sync.dma_start(runs[:, 0:RUN], gain[0:1, :].rearrange("o (n m) -> (o n) m", m=RUN))
+        nc.sync.dma_start(runs[:, RUN : 2 * RUN], shift[0:1, :].rearrange("o (n m) -> (o n) m", m=RUN))
+        w1_raw0 = keep.tile([P, 4, H], F32, name="w1_raw0")
+        nc.sync.dma_start(w1_raw0[:], w1_rows(0))
+        offsets = keep.tile([P, S // 16], U16, name="offsets")
+        nc.sync.dma_start(offsets[:], offs)
+        wsum_cols = keep.tile([P, 4], F32, name="wsum_cols")
+        nc.sync.dma_start(wsum_cols[:], wsum.rearrange("(p t) o -> p (t o)", t=4))
+
+        zeros = shared.tile([P, P - RUN], F32, name="zeros", offset=4 * T + 4 * N + 4 * S + 16 * H - 2 * P)
+        nc.vector.memset(zeros[:], 0.0)
+        scale_table = scale_space.tile([P, T], U8, name="scale_table", offset=0)
+        nc.vector.memset(scale_table[:].bitcast(I32), 0)
+        for o in range(PASSES):
+            nc.sync.dma_start(scale_table[4 * o : P : 8, :].bitcast(I32), x_scales[o].bitcast(I32))
+        nc.vector.tensor_copy(runs[:, 2 * RUN :], zeros[:])
+        w1_raw1 = shared.tile([P, 4, H], F32, name="w1_raw1", offset=4 * T + 4 * N + 4 * S)
+        nc.sync.dma_start(w1_raw1[:], w1_rows(1))
+        x_table0 = shared.tile([P, T], I32, name="x_table0", offset=4 * T + 4 * N + 4 * S + 16 * H)
+        nc.sync.dma_start(x_table0[:], x_words[0].rearrange("p c b -> p (c b)").bitcast(I32))
+
+        ident = keep.tile([P, P], F32, name="ident")
+        make_identity(nc, ident[:])
+
+        row_table = keep.tile([P, T], F32, name="row_table")
+        for b in range(RUN // 4):
+            turned = bank(b, [P, 4, P])
+            for a in range(4):
+                m = 4 * b + a
+                nc.tensor.transpose(turned[:, a, :], runs[:, m : m + P], ident[:])
+            copier("ssssssss"[b])(
+                row_table[:].rearrange("p (n m) -> p n m", m=RUN)[:, :, 4 * b : 4 * b + 4],
+                turned[:].rearrange("p a n -> p n a"),
+            )
+
+        wsum_rows = bank(5, [P, 4, P])
         for t in range(4):
             nc.tensor.transpose(wsum_rows[:, t, :], wsum_cols[:, t : t + 1].to_broadcast([P, P]), ident[:])
 
@@ -91,15 +92,15 @@ def tile_picked_zdq_mlprelu_po_kernel(
         nc.vector.tensor_copy(picked_scales[:], scale_table[:].indirect(offsets[:]))
         x_plane = keep.tile([P, S], U8, name="x_plane", align_bytes=64)
         nc.vector.tensor_copy(x_plane[:].bitcast(I32), picked_scales[:].bitcast(I32))
-        for o in range(PASSES):
-            for r in range(1, 4):
+        for r in range(1, 4):
+            for o in range(PASSES):
                 nc.sync.dma_start(
                     x_plane[4 * o + r : P : 32, :].bitcast(I32), picked_scales[8 * r + 4 * o : P : 32, :].bitcast(I32)
                 )
 
         grouped = [
-            second_space.tile([P, 4 * H], BF16, name="w1_grouped0", align_bytes=64, offset=4 * T - 64),
-            second_space.tile([P, 4 * H], BF16, name="w1_grouped1", align_bytes=64, offset=8 * T + 4 * N + 4 * S + 16 * H),
+            shared.tile([P, 4 * H], BF16, name="w1_grouped0", align_bytes=64, offset=4 * T - 64),
+            shared.tile([P, 4 * H], BF16, name="w1_grouped1", align_bytes=64, offset=8 * T + 4 * N + 4 * S + 16 * H),
         ]
         w1_codes = [
             scale_space.tile([P, H], U32, name="w1_codes0", align_bytes=64, offset=0),
@@ -107,7 +108,7 @@ def tile_picked_zdq_mlprelu_po_kernel(
         ]
         w1_plane = [keep.tile([P, H], U8, name="w1_plane%d" % o, align_bytes=64) for o in range(PASSES)]
         for o, raw in enumerate([w1_raw0, w1_raw1]):
-            nc.scalar.copy(
+            copier("vs"[o])(
                 grouped[o][:].rearrange("p (u m e j) -> p u m j e", u=2, e=2, j=4),
                 raw[:].rearrange("p j (m u e) -> p u m j e", u=2, e=2),
             )
@@ -117,11 +118,11 @@ def tile_picked_zdq_mlprelu_po_kernel(
 
         quantise_w1(0)
 
-        x_table1 = second_space.tile([P, T], I32, name="x_table1", offset=0)
+        x_table1 = shared.tile([P, T], I32, name="x_table1", offset=0)
         nc.sync.dma_start(x_table1[:], x_words[1].rearrange("p c b -> p (c b)").bitcast(I32))
 
         picked_rows = [
-            second_space.tile([P, S // 2], F32, name="picked_rows%d" % half, offset=4 * T + 2 * S * half) for half in range(2)
+            shared.tile([P, S // 2], F32, name="picked_rows%d" % half, offset=4 * T + 2 * S * half) for half in range(2)
         ]
         for half in range(2):
             nc.vector.tensor_copy(
@@ -129,29 +130,39 @@ def tile_picked_zdq_mlprelu_po_kernel(
             )
 
         quantise_w1(1)
-        w2_raw = second_space.tile([P, N], I32, name="w2_raw", offset=8 * T + 4 * N + 4 * S + 16 * H)
+        w2_raw = shared.tile([P, N], I32, name="w2_raw", offset=8 * T + 4 * N + 4 * S + 16 * H)
         nc.sync.dma_start(w2_raw[:], w2_words[0].rearrange("p c b -> p (c b)").bitcast(I32))
-        x_code0 = keep.tile([P, S], U32, name="x_code0", align_bytes=64)
-        nc.vector.tensor_copy(x_code0[:], x_table0[:].bitcast(U32).indirect(offsets[:]))
 
-        w2_raw_scales = second_space.tile([P, N], U8, name="w2_raw_scales", offset=4 * T + 4 * N + 4 * S + 20 * H)
+        def gather_words(table, o, pieces):
+            width = S // pieces
+            tiles = [keep.tile([P, width], U32, name="x_code%d_%d" % (o, a), align_bytes=64) for a in range(pieces)]
+            for a, tile in enumerate(tiles):
+                nc.vector.tensor_copy(
+                    tile[:], table[:].bitcast(U32).indirect(offsets[:, width // 16 * a : width // 16 * (a + 1)])
+                )
+            return tiles
+
+        x_code = [gather_words(x_table0, 0, 1)]
+
+        w2_raw_scales = shared.tile([P, N], U8, name="w2_raw_scales", offset=4 * T + 4 * N + 4 * S + 20 * H)
         nc.vector.memset(w2_raw_scales[:].bitcast(I32), 0)
         for q in range(4):
             nc.sync.dma_start(
                 w2_raw_scales[32 * q : 32 * q + 4, :].bitcast(I32), w2_scales[0, 4 * q : 4 * q + 4, :].bitcast(I32)
             )
 
-        factors = second_space.tile([P, TILES, 2], F32, name="factors", offset=4 * T + 8 * N + 4 * S)
+        factors = shared.tile([P, TILES, 2], F32, name="factors", offset=4 * T + 8 * N + 4 * S)
+
         def turn_factors(half):
-            turned = bank(len(EARLY) - 2, [P, 4, P])
+            turned = bank(4, [P, 4, P])
             for a in range(4):
                 nc.tensor.transpose(turned[:, a, :], picked_rows[half][:, P * a : P * (a + 1)], ident[:])
-            nc.scalar.copy(factors[:, 4 * half : 4 * half + 4, :], turned[:, :, P // 2 - 1 : P : P // 2])
+            nc.scalar.copy(factors[:, 4 * half : 4 * half + 4, :], turned[:, :, 0 : 2 * RUN : RUN])
 
         offsets_term, turned_sum = {}, {}
         turn_factors(0)
         for jt in range(TILES):
-            if jt == len(SUMMED):
+            if jt == 2:
                 turn_factors(1)
             term = keep.tile([P, H], F32, name="term%d" % jt)
             if jt in SUMMED:
@@ -178,42 +189,46 @@ def tile_picked_zdq_mlprelu_po_kernel(
                 )
             offsets_term[jt] = term
 
-        x_code1 = [keep.tile([P, S // 2], U32, name="x_code1%d" % half, align_bytes=64) for half in range(2)]
-        for half in range(2):
-            nc.vector.tensor_copy(
-                x_code1[half][:], x_table1[:].bitcast(U32).indirect(offsets[:, S // 32 * half : S // 32 * (half + 1)])
-            )
+        x_code.append(gather_words(x_table1, 1, 4))
 
-        w2_codes = second_space.tile([P, N], I32, name="w2_codes", align_bytes=64, offset=0)
+        w2_codes = shared.tile([P, N], I32, name="w2_codes", align_bytes=64, offset=0)
         nc.gpsimd.tensor_copy(
             w2_codes[:].rearrange("p (t m) -> p t m", t=4), w2_raw[:].rearrange("p (m t) -> p t m", t=4)
         )
-        w2_plane = second_space.tile([P, N], U8, name="w2_plane", align_bytes=64, offset=4 * N)
+        w2_plane = shared.tile([P, N], U8, name="w2_plane", align_bytes=64, offset=4 * N)
         nc.gpsimd.tensor_copy(
             w2_plane[:].rearrange("p (t m) -> p t m", t=4), w2_raw_scales[:].rearrange("p (m t) -> p t m", t=4)
         )
 
         def x_codes(jt, o):
-            half, place = divmod(jt, TILES // 2)
-            if o == 0:
-                return x_code0[:, P * jt : P * (jt + 1)]
-            return x_code1[half][:, P * place : P * (place + 1)]
+            piece, place = divmod(jt, TILES // len(x_code[o]))
+            return x_code[o][piece][:, P * place : P * (place + 1)]
 
-        out_plane = keep.tile([P, S], U8, name="out_plane", align_bytes=64)
+        out_plane = keep.tile([P, 2 * P], U8, name="out_plane", align_bytes=64)
         out_codes = keep.tile([P, S], U32, name="out_codes", align_bytes=64)
         out_rows = out_0.rearrange("(p t) j -> p t j", t=4)
         out_words = out_1[0].rearrange("p c b -> p (c b)").bitcast(I32)
 
         sums, pre, turned_pairs, products, result = {}, {}, {}, {}, {}
-        hidden_mx, rounded = {}, {}
-        hidden = keep.tile([P, 4 * S], BF16, name="hidden", align_bytes=64)
+        hidden_mx = {}
+        stage = ctx.enter_context(tc.tile_pool(name="stage", bufs=1))
+        hidden = {}
+
+        def hidden_tile(first, count):
+            tile = stage.tile([P, 4 * P * count], BF16, name="hidden%d" % first, align_bytes=64, offset=8 * P * first)
+            for a in range(count):
+                hidden[first + a] = (tile, a)
+
+        def hidden_cols(first, count):
+            tile, a = hidden[first]
+            return tile[:, 4 * P * a : 4 * P * (a + count)]
+
+        for first, count in CHUNKS:
+            hidden_tile(first, count)
         for first, count in STORES:
             res = keep.tile([P, 4, P * count], F32, name="res%d" % first)
             for a in range(count):
                 result[first + a] = (res, a)
-
-        def copier(engine):
-            return {"s": nc.scalar.copy, "v": nc.vector.tensor_copy}[engine]
 
         def product_pass(jt, o, b=None):
             if o == 0:
@@ -269,7 +284,7 @@ def tile_picked_zdq_mlprelu_po_kernel(
             turned_pairs[first] = (b, turned)
 
         def rectify(first, count=1, engine="v"):
-            h = hidden[:, 4 * P * first : 4 * P * (first + count)]
+            h = hidden_cols(first, count)
             if first in SUMMED:
                 b, turned = turned_sum[first]
                 target, source = h.rearrange("p (j t) -> p j t", t=4), turned[:].rearrange("p t j -> p j t")
@@ -285,7 +300,7 @@ def tile_picked_zdq_mlprelu_po_kernel(
         def quantise_hidden(first, count=1):
             codes = keep.tile([P, P * count], U32, name="h_codes%d" % first, align_bytes=64)
             plane = keep.tile([P, P * count], U8, name="h_plane%d" % first, align_bytes=64)
-            nc.vector.quantize_mx(out=codes[:].bitcast(FP8X4), scales=plane[:], in_=hidden[:, 4 * P * first : 4 * P * (first + count)])
+            nc.vector.quantize_mx(out=codes[:].bitcast(FP8X4), scales=plane[:], in_=hidden_cols(first, count))
             for a in range(count):
                 hidden_mx[first + a] = (codes[:, P * a : P * (a + 1)], plane[:, P * a : P * (a + 1)])
 
@@ -314,17 +329,10 @@ def tile_picked_zdq_mlprelu_po_kernel(
             res, a = result[first]
             nc.sync.dma_start(out_rows[:, :, P * first : P * first + res[:].shape[2]], res[:])
 
-        def rounded_tile(first, count, on=None):
-            if on is None:
-                tile = keep.tile([P, 4 * P * count], BF16, name="rounded%d" % first, align_bytes=64)
-            else:
-                tile = stage.tile([P, 4 * P * count], BF16, name="rounded%d" % first, align_bytes=64, offset=8 * P * on)
-            for a in range(count):
-                rounded[first + a] = (tile, a)
+        rounded = keep.tile([P, 4 * S], BF16, name="rounded", align_bytes=64)
 
         def rounded_cols(first, count):
-            tile, a = rounded[first]
-            return tile[:, 4 * P * a : 4 * P * (a + count)]
+            return rounded[:, 4 * P * first : 4 * P * (first + count)]
 
         def round_bank(jt, engine="s"):
             b, acc = products[jt]
@@ -355,7 +363,7 @@ def tile_picked_zdq_mlprelu_po_kernel(
             cols = slice(P * first, P * (first + count))
             nc.vector.quantize_mx(
                 out=out_codes[:, cols].bitcast(FP8X4),
-                scales=out_plane[:, cols],
+                scales=out_plane[4 * (first // 2) : P, P * (first % 2) : P * (first % 2 + count)],
                 in_=rounded_cols(first, count),
             )
 
@@ -365,7 +373,6 @@ def tile_picked_zdq_mlprelu_po_kernel(
 
         for b, jt in enumerate(EARLY):
             product_pass(jt, 0, b)
-        rounded_tile(0, 8)
         close(0)
         close(1)
         close(2)
@@ -434,4 +441,7 @@ def tile_picked_zdq_mlprelu_po_kernel(
 
         for q in range(4):
             queue = nc.sync if q % 2 == 0 else nc.scalar
-            queue.dma_start(out_2[0, 4 * q : 4 * q + 4, :].bitcast(I32), out_plane[32 * q : 32 * q + 4, :].bitcast(I32))
+            queue.dma_start(
+                out_2[0, 4 * q : 4 * q + 4, :].bitcast(I32).rearrange("r (c j) -> c r j", c=4),
+                out_plane[32 * q : 32 * q + 16, :].bitcast(I32),
+            )

@@ -51,7 +51,7 @@ def tile_picked_zdq_mlprelu_po_kernel(
         runs = keep.tile([P, RUN + P], F32, name="runs")
         nc.sync.dma_start(runs[:, 0:RUN], gain[0:1, :].rearrange("o (n m) -> (o n) m", m=RUN))
         nc.sync.dma_start(runs[:, RUN : 2 * RUN], shift[0:1, :].rearrange("o (n m) -> (o n) m", m=RUN))
-        w1_raw0 = keep.tile([P, 4, H], F32, name="w1_raw0")
+        w1_raw0 = keep.tile([P, 4, H], F32, name="w1_raw0", align_bytes=256)
         nc.sync.dma_start(w1_raw0[:], w1_rows(0))
         offsets = keep.tile([P, S // 16], U16, name="offsets")
         nc.sync.dma_start(offsets[:], offs)
@@ -60,14 +60,14 @@ def tile_picked_zdq_mlprelu_po_kernel(
 
         zeros = shared.tile([P, P - RUN], F32, name="zeros", offset=4 * T + 4 * N + 4 * S + 16 * H - 2 * P)
         nc.vector.memset(zeros[:], 0.0)
-        scale_table = scale_space.tile([P, T], U8, name="scale_table", offset=0)
+        scale_table = scale_space.tile([P, T], U8, name="scale_table", align_bytes=256, offset=0)
         nc.vector.memset(scale_table[:].bitcast(I32), 0)
         for o in range(PASSES):
             nc.sync.dma_start(scale_table[4 * o : P : 8, :].bitcast(I32), x_scales[o].bitcast(I32))
         nc.vector.tensor_copy(runs[:, 2 * RUN :], zeros[:])
-        w1_raw1 = shared.tile([P, 4, H], F32, name="w1_raw1", offset=4 * T + 4 * N + 4 * S)
+        w1_raw1 = shared.tile([P, 4, H], F32, name="w1_raw1", align_bytes=256, offset=4 * T + 4 * N + 4 * S)
         nc.sync.dma_start(w1_raw1[:], w1_rows(1))
-        x_table0 = shared.tile([P, T], I32, name="x_table0", offset=4 * T + 4 * N + 4 * S + 16 * H)
+        x_table0 = shared.tile([P, T], I32, name="x_table0", align_bytes=256, offset=4 * T + 4 * N + 4 * S + 16 * H)
         nc.sync.dma_start(x_table0[:], x_words[0].rearrange("p c b -> p (c b)").bitcast(I32))
 
         ident = keep.tile([P, P], F32, name="ident")
@@ -118,7 +118,7 @@ def tile_picked_zdq_mlprelu_po_kernel(
 
         quantise_w1(0)
 
-        x_table1 = shared.tile([P, T], I32, name="x_table1", offset=0)
+        x_table1 = shared.tile([P, T], I32, name="x_table1", align_bytes=256, offset=0)
         nc.sync.dma_start(x_table1[:], x_words[1].rearrange("p c b -> p (c b)").bitcast(I32))
 
         picked_rows = [
@@ -130,7 +130,7 @@ def tile_picked_zdq_mlprelu_po_kernel(
             )
 
         quantise_w1(1)
-        w2_raw = shared.tile([P, N], I32, name="w2_raw", offset=8 * T + 4 * N + 4 * S + 16 * H)
+        w2_raw = shared.tile([P, N], I32, name="w2_raw", align_bytes=256, offset=8 * T + 4 * N + 4 * S + 16 * H)
         nc.sync.dma_start(w2_raw[:], w2_words[0].rearrange("p c b -> p (c b)").bitcast(I32))
 
         def gather_words(table, o, pieces):
@@ -205,7 +205,7 @@ def tile_picked_zdq_mlprelu_po_kernel(
             return x_code[o][piece][:, P * place : P * (place + 1)]
 
         out_plane = keep.tile([P, 2 * P], U8, name="out_plane", align_bytes=64)
-        out_codes = keep.tile([P, S], U32, name="out_codes", align_bytes=64)
+        out_codes = keep.tile([P, S], U32, name="out_codes", align_bytes=256)
         out_rows = out_0.rearrange("(p t) j -> p t j", t=4)
         out_words = out_1[0].rearrange("p c b -> p (c b)").bitcast(I32)
 
@@ -226,7 +226,7 @@ def tile_picked_zdq_mlprelu_po_kernel(
         for first, count in CHUNKS:
             hidden_tile(first, count)
         for first, count in STORES:
-            res = keep.tile([P, 4, P * count], F32, name="res%d" % first)
+            res = keep.tile([P, 4, P * count], F32, name="res%d" % first, align_bytes=256)
             for a in range(count):
                 result[first + a] = (res, a)
 

@@ -204,7 +204,7 @@ def tile_picked_zdq_mlprelu_po_kernel(
             piece, place = divmod(jt, TILES // len(x_code[o]))
             return x_code[o][piece][:, P * place : P * (place + 1)]
 
-        out_plane = keep.tile([P, 2 * P], U8, name="out_plane", align_bytes=64)
+        out_plane = keep.tile([P, 4 * P], U8, name="out_plane", align_bytes=64)
         out_codes = keep.tile([P, S], U32, name="out_codes", align_bytes=256)
         out_rows = out_0.rearrange("(p t) j -> p t j", t=4)
         out_words = out_1[0].rearrange("p c b -> p (c b)").bitcast(I32)
@@ -363,7 +363,7 @@ def tile_picked_zdq_mlprelu_po_kernel(
             cols = slice(P * first, P * (first + count))
             nc.vector.quantize_mx(
                 out=out_codes[:, cols].bitcast(FP8X4),
-                scales=out_plane[4 * (first // 2) : P, P * (first % 2) : P * (first % 2 + count)],
+                scales=out_plane[4 * (first // 4) : P, P * (first % 4) : P * (first % 4 + count)],
                 in_=rounded_cols(first, count),
             )
 
@@ -393,9 +393,9 @@ def tile_picked_zdq_mlprelu_po_kernel(
         combine(4)
         close(6, 2)
         quantise_hidden(0)
+        close(7, 4)
         second_layer(0, 3)
         rectify(3, 1)
-        close(7, 4)
         quantise_hidden(1)
         second_layer(1, 6)
         empty(0)
@@ -442,6 +442,6 @@ def tile_picked_zdq_mlprelu_po_kernel(
         for q in range(4):
             queue = nc.sync if q % 2 == 0 else nc.scalar
             queue.dma_start(
-                out_2[0, 4 * q : 4 * q + 4, :].bitcast(I32).rearrange("r (c j) -> c r j", c=4),
-                out_plane[32 * q : 32 * q + 16, :].bitcast(I32),
+                out_2[0, 4 * q : 4 * q + 4, :].bitcast(I32).rearrange("r (c j) -> c r j", c=2),
+                out_plane[32 * q : 32 * q + 8, :].bitcast(I32),
             )

@@ -303,6 +303,7 @@ def tile_picked_zdq_mlprelu_po_kernel(
             nc.vector.quantize_mx(out=codes[:].bitcast(FP8X4), scales=plane[:], in_=hidden_cols(first, count))
             for a in range(count):
                 hidden_mx[first + a] = (codes[:, P * a : P * (a + 1)], plane[:, P * a : P * (a + 1)])
+            hidden_mx[first, count] = (codes[:], plane[:])
 
         def second_layer(first, *banks):
             for jt, b in enumerate(banks, first):
@@ -319,6 +320,29 @@ def tile_picked_zdq_mlprelu_po_kernel(
                         stop=True,
                     )
                 products[jt] = (b, acc)
+
+        def second_layer_wide(first, *banks):
+            codes, plane = hidden_mx[first, 2]
+            res, a = result[first]
+            for half, b in enumerate(banks):
+                acc = bank(b, [P, 2, 2 * P])
+                for t in range(2 * half, 2 * half + 2):
+                    nc.tensor.matmul_mx(
+                        out=acc[:, t % 2, :],
+                        lhsT=w2_codes[:, P * t : P * (t + 1)].bitcast(FP8X4),
+                        lhsT_scale=w2_plane[:, P * t : P * (t + 1)],
+                        rhs=codes.bitcast(FP8X4),
+                        rhs_scale=plane,
+                        start=True,
+                        stop=True,
+                    )
+                products[first + half] = (b, acc)
+
+        def empty_half(first, half):
+            res, a = result[first]
+            rows = slice(2 * half, 2 * half + 2)
+            nc.scalar.copy(res[:, rows, :], products[first + half][1][:])
+            nc.sync.dma_start(out_rows[:, rows, P * first : P * (first + 2)], res[:, rows, :])
 
         def empty(jt, engine="s"):
             b, acc = products[jt]
@@ -417,17 +441,17 @@ def tile_picked_zdq_mlprelu_po_kernel(
         round_bank(1)
         round_bank(2)
         quantise_hidden(4, 2)
-        second_layer(4, 2, 3)
+        second_layer_wide(4, 2, 3)
         rectify(6, 2)
         quantise_result(0, 2)
+        store_words(0, 2)
         quantise_hidden(6, 2)
         second_layer(6, 4, 7)
         round_result(3)
-        empty(4)
-        empty(5)
-        store(4)
+        empty_half(4, 0)
+        empty_half(4, 1)
         quantise_result(2, 2)
-        store_words(0, 4)
+        store_words(2, 4)
         empty(6, "v")
         round_result(4, 2)
         empty(7)
@@ -435,9 +459,10 @@ def tile_picked_zdq_mlprelu_po_kernel(
         round_bank(7)
         round_result(6)
         quantise_result(4, 2)
-        store_words(4, 6)
-        quantise_result(6, 2)
-        store_words(6, 8)
+        quantise_result(6)
+        store_words(4, 7)
+        quantise_result(7)
+        store_words(7, 8)
 
         for q in range(4):
             queue = nc.sync if q % 2 == 0 else nc.scalar

@@ -465,8 +465,7 @@ def tile_picked_zdq_mlprelu_po_kernel(
         store_words(7, 8)
 
         for q in range(4):
-            queue = nc.sync if q % 2 == 0 else nc.scalar
-            queue.dma_start(
+            nc.scalar.dma_start(
                 out_2[0, 4 * q : 4 * q + 4, :].bitcast(I32).rearrange("r (c j) -> c r j", c=2),
                 out_plane[32 * q : 32 * q + 8, :].bitcast(I32),
             )

from contextlib import ExitStack

import concourse.mybir as mybir
from concourse.masks import make_identity

K, T, S, H, N = 1024, 4096, 1024, 512, 512
FLOPS = 2 * K * H * S + 2 * H * N * S
BYTES = K * T + K * T // 32 + 4 * K * H + 8 * T + 4 * H + H * N + H * N // 32 + 128 * 64 * 2 + 4 * N * S + N * S + N * S // 32

F32 = mybir.dt.float32
BF16 = mybir.dt.bfloat16
I32 = mybir.dt.int32
U32 = mybir.dt.uint32
U16 = mybir.dt.uint16
U8 = mybir.dt.uint8
FP8X4 = mybir.dt.float8_e4m3fn_x4
MULT = mybir.AluOpType.mult
ADD = mybir.AluOpType.add
COPY = mybir.ActivationFunctionType.Copy
RELU = mybir.ActivationFunctionType.Relu

P = 128
PASSES = K // 512
TILES = S // P
RUN = T // P
SUMMED = [0, 1]
EARLY = [0, 1, 2, 3, 4, 5]
CHUNKS = [(0, 1), (1, 1), (2, 2), (4, 2), (6, 2)]
STORES = [(0, 1), (1, 1), (2, 2), (4, 2), (6, 2)]


def tile_picked_zdq_mlprelu_po_kernel(
    tc, x_words, x_scales, w1, gain, shift, wsum, w2_words, w2_scales, offs, out_0, out_1, out_2
):
    nc = tc.nc
    with ExitStack() as ctx:
        keep = ctx.enter_context(tc.tile_pool(name="keep", bufs=1))
        scale_space = ctx.enter_context(tc.tile_pool(name="scale_space", bufs=1))
        shared = ctx.enter_context(tc.tile_pool(name="shared", bufs=1))
        psum = ctx.enter_context(tc.psum_pool(name="psum", bufs=1))

        def bank(b, shape):
            return psum.tile(shape, F32, name="bank%d" % b, tag="bank%d" % b)

        def copier(engine):
            return {"s": nc.scalar.copy, "v": nc.vector.tensor_copy}[engine]

        def w1_rows(o):
            return w1[512 * o : 512 * (o + 1), :].rearrange("(p j) c -> p j c", j=4)

        runs = keep.tile([P, RUN + P], F32, name="runs")
        nc.sync.dma_start(runs[:, 0:RUN], gain[0:1, :].rearrange("o (n m) -> (o n) m", m=RUN))
        nc.sync.dma_start(runs[:, RUN : 2 * RUN], shift[0:1, :].rearrange("o (n m) -> (o n) m", m=RUN))
        w1_raw0 = keep.tile([P, 4, H], F32, name="w1_raw0", align_bytes=256)
        nc.sync.dma_start(w1_raw0[:], w1_rows(0))
        offsets = keep.tile([P, S // 16], U16, name="offsets")
        nc.sync.dma_start(offsets[:], offs)
        wsum_cols = keep.tile([P, 4], F32, name="wsum_cols")
        nc.sync.dma_start(wsum_cols[:], wsum.rearrange("(p t) o -> p (t o)", t=4))

        zeros = shared.tile([P, P - RUN], F32, name="zeros", offset=4 * T + 4 * N + 4 * S + 16 * H - 2 * P)
        nc.vector.memset(zeros[:], 0.0)
        scale_table = scale_space.tile([P, T], U8, name="scale_table", align_bytes=256, offset=0)
        nc.vector.memset(scale_table[:].bitcast(I32), 0)
        for o in range(PASSES):
            nc.sync.dma_start(scale_table[4 * o : P : 8, :].bitcast(I32), x_scales[o].bitcast(I32))
        nc.vector.tensor_copy(runs[:, 2 * RUN :], zeros[:])
        w1_raw1 = shared.tile([P, 4, H], F32, name="w1_raw1", align_bytes=256, offset=4 * T + 4 * N + 4 * S)
        nc.sync.dma_start(w1_raw1[:], w1_rows(1))
        x_table0 = shared.tile([P, T], I32, name="x_table0", align_bytes=256, offset=4 * T + 4 * N + 4 * S + 16 * H)
        nc.sync.dma_start(x_table0[:], x_words[0].rearrange("p c b -> p (c b)").bitcast(I32))

        ident = keep.tile([P, P], F32, name="ident")
        make_identity(nc, ident[:])

        row_table = keep.tile([P, T], F32, name="row_table")
        for b in range(RUN // 4):
            turned = bank(b, [P, 4, P])
            for a in range(4):
                m = 4 * b + a
                nc.tensor.transpose(turned[:, a, :], runs[:, m : m + P], ident[:])
            copier("ssssssss"[b])(
                row_table[:].rearrange("p (n m) -> p n m", m=RUN)[:, :, 4 * b : 4 * b + 4],
                turned[:].rearrange("p a n -> p n a"),
            )

        wsum_rows = bank(5, [P, 4, P])
        for t in range(4):
            nc.tensor.transpose(wsum_rows[:, t, :], wsum_cols[:, t : t + 1].to_broadcast([P, P]), ident[:])

        picked_scales = keep.tile([P, S], U8, name="picked_scales")
        nc.vector.tensor_copy(picked_scales[:], scale_table[:].indirect(offsets[:]))
        x_plane = keep.tile([P, S], U8, name="x_plane", align_bytes=64)
        nc.vector.tensor_copy(x_plane[:].bitcast(I32), picked_scales[:].bitcast(I32))
        for r in range(1, 4):
            for o in range(PASSES):
                nc.sync.dma_start(
                    x_plane[4 * o + r : P : 32, :].bitcast(I32), picked_scales[8 * r + 4 * o : P : 32, :].bitcast(I32)
                )

        grouped = [
            shared.tile([P, 4 * H], BF16, name="w1_grouped0", align_bytes=64, offset=4 * T - 64),
            shared.tile([P, 4 * H], BF16, name="w1_grouped1", align_bytes=64, offset=8 * T + 4 * N + 4 * S + 16 * H),
        ]
        w1_codes = [
            scale_space.tile([P, H], U32, name="w1_codes0", align_bytes=64, offset=0),
            keep.tile([P, H], U32, name="w1_codes1", align_bytes=64),
        ]
        w1_plane = [keep.tile([P, H], U8, name="w1_plane%d" % o, align_bytes=64) for o in range(PASSES)]
        for o, raw in enumerate([w1_raw0, w1_raw1]):
            copier("vs"[o])(
                grouped[o][:].rearrange("p (u m e j) -> p u m j e", u=2, e=2, j=4),
                raw[:].rearrange("p j (m u e) -> p u m j e", u=2, e=2),
            )

        def quantise_w1(o):
            nc.vector.quantize_mx(out=w1_codes[o][:].bitcast(FP8X4), scales=w1_plane[o][:], in_=grouped[o][:])

        quantise_w1(0)

        x_table1 = shared.tile([P, T], I32, name="x_table1", align_bytes=256, offset=0)
        nc.sync.dma_start(x_table1[:], x_words[1].rearrange("p c b -> p (c b)").bitcast(I32))

        picked_rows = [
            shared.tile([P, S // 2], F32, name="picked_rows%d" % half, offset=4 * T + 2 * S * half) for half in range(2)
        ]
        for half in range(2):
            nc.vector.tensor_copy(
                picked_rows[half][:], row_table[:].indirect(offsets[:, S // 32 * half : S // 32 * (half + 1)])
            )

        quantise_w1(1)
        w2_raw = shared.tile([P, N], I32, name="w2_raw", align_bytes=256, offset=8 * T + 4 * N + 4 * S + 16 * H)
        nc.sync.dma_start(w2_raw[:], w2_words[0].rearrange("p c b -> p (c b)").bitcast(I32))

        def gather_words(table, o, pieces):
            width = S // pieces
            tiles = [keep.tile([P, width], U32, name="x_code%d_%d" % (o, a), align_bytes=64) for a in range(pieces)]
            for a, tile in enumerate(tiles):
                nc.vector.tensor_copy(
                    tile[:], table[:].bitcast(U32).indirect(offsets[:, width // 16 * a : width // 16 * (a + 1)])
                )
            return tiles

        x_code = [gather_words(x_table0, 0, 1)]

        w2_raw_scales = shared.tile([P, N], U8, name="w2_raw_scales", offset=4 * T + 4 * N + 4 * S + 20 * H)
        nc.vector.memset(w2_raw_scales[:].bitcast(I32), 0)
        for q in range(4):
            nc.sync.dma_start(
                w2_raw_scales[32 * q : 32 * q + 4, :].bitcast(I32), w2_scales[0, 4 * q : 4 * q + 4, :].bitcast(I32)
            )

        factors = shared.tile([P, TILES, 2], F32, name="factors", offset=4 * T + 8 * N + 4 * S)

        def turn_factors(half):
            turned = bank(4, [P, 4, P])
            for a in range(4):
                nc.tensor.transpose(turned[:, a, :], picked_rows[half][:, P * a : P * (a + 1)], ident[:])
            nc.scalar.copy(factors[:, 4 * half : 4 * half + 4, :], turned[:, :, 0 : 2 * RUN : RUN])

        offsets_term, turned_sum = {}, {}
        turn_factors(0)
        for jt in range(TILES):
            if jt == 2:
                turn_factors(1)
            term = keep.tile([P, H], F32, name="term%d" % jt)
            if jt in SUMMED:
                nc.scalar.activation(
                    term[:], wsum_rows[:].rearrange("p t m -> p (t m)"), COPY, scale=factors[:, jt, 1:2]
                )
                b = len(EARLY) + SUMMED.index(jt)
                turned_sum[jt] = (b, bank(b, [P, 4, P]))
                for t in range(4):
                    nc.tensor.matmul(
                        turned_sum[jt][1][:, t, :],
                        term[:, P * t : P * (t + 1)],
                        ident[:],
                        start=t == 0,
                        stop=False,
                        is_transpose=True,
                    )
            else:
                nc.scalar.activation(
                    term[:].rearrange("p (u m e) -> p u m e", u=2, e=2),
                    wsum_rows[:].rearrange("p (u e) m -> p u m e", u=2),
                    COPY,
                    scale=factors[:, jt, 1:2],
                )
            offsets_term[jt] = term

        x_code.append(gather_words(x_table1, 1, 4))

        w2_codes = shared.tile([P, N], I32, name="w2_codes", align_bytes=64, offset=0)
        nc.gpsimd.tensor_copy(
            w2_codes[:].rearrange("p (t m) -> p t m", t=4), w2_raw[:].rearrange("p (m t) -> p t m", t=4)
        )
        w2_plane = shared.tile([P, N], U8, name="w2_plane", align_bytes=64, offset=4 * N)
        nc.gpsimd.tensor_copy(
            w2_plane[:].rearrange("p (t m) -> p t m", t=4), w2_raw_scales[:].rearrange("p (m t) -> p t m", t=4)
        )

        def x_codes(jt, o):
            piece, place = divmod(jt, TILES // len(x_code[o]))
            return x_code[o][piece][:, P * place : P * (place + 1)]

        out_plane = keep.tile([P, 4 * P], U8, name="out_plane", align_bytes=64)
        out_codes = keep.tile([P, S], U32, name="out_codes", align_bytes=256)
        out_rows = out_0.rearrange("(p t) j -> p t j", t=4)
        out_words = out_1[0].rearrange("p c b -> p (c b)").bitcast(I32)

        sums, pre, turned_pairs, products, result = {}, {}, {}, {}, {}
        hidden_mx = {}
        stage = ctx.enter_context(tc.tile_pool(name="stage", bufs=1))
        hidden = {}

        def hidden_tile(first, count):
            tile = stage.tile([P, 4 * P * count], BF16, name="hidden%d" % first, align_bytes=64, offset=8 * P * first)
            for a in range(count):
                hidden[first + a] = (tile, a)

        def hidden_cols(first, count):
            tile, a = hidden[first]
            return tile[:, 4 * P * a : 4 * P * (a + count)]

        for first, count in CHUNKS:
            hidden_tile(first, count)
        for first, count in STORES:
            res = keep.tile([P, 4, P * count], F32, name="res%d" % first, align_bytes=256)
            for a in range(count):
                result[first + a] = (res, a)

        def product_pass(jt, o, b=None):
            if o == 0:
                sums[jt] = (b, bank(b, [P, H]))
            nc.tensor.matmul_mx(
                out=sums[jt][1][:],
                lhsT=x_codes(jt, o).bitcast(FP8X4),
                lhsT_scale=x_plane[4 * o : P, P * jt : P * (jt + 1)],
                rhs=w1_codes[o][:].bitcast(FP8X4),
                rhs_scale=w1_plane[o][:],
                start=o == 0,
                stop=o == 1,
            )

        def close(jt, b=None):
            if jt not in EARLY:
                product_pass(jt, 0, b)
            product_pass(jt, 1)

        def combine(jt):
            b, y = sums[jt]
            if jt in SUMMED:
                pre[jt] = keep.tile([P, H], F32, name="scaled%d" % jt)
                nc.scalar.activation(
                    pre[jt][:].rearrange("p (u e m) -> p u e m", u=2, e=2),
                    y[:].rearrange("p (u m e) -> p u e m", u=2, e=2),
                    COPY,
                    scale=factors[:, jt, 0:1],
                )
            else:
                pre[jt] = keep.tile([P, H], BF16, name="pre%d" % jt)
                nc.vector.scalar_tensor_tensor(
                    out=pre[jt][:], in0=y[:], scalar=factors[:, jt, 0:1], in1=offsets_term[jt][:], op0=MULT, op1=ADD
                )

        def turn(first, count=1, b=None):
            if first in SUMMED:
                for t in range(4):
                    nc.tensor.matmul(
                        turned_sum[first][1][:, t, :],
                        pre[first][:, P * t : P * (t + 1)],
                        ident[:],
                        start=False,
                        stop=t == 3,
                        is_transpose=True,
                    )
                return
            turned = bank(b, [P, 2, P * count])
            for a in range(count):
                words = pre[first + a][:].bitcast(F32)
                for u in range(2):
                    nc.tensor.transpose(turned[:, u, P * a : P * (a + 1)], words[:, P * u : P * (u + 1)], ident[:])
            turned_pairs[first] = (b, turned)

        def rectify(first, count=1, engine="v"):
            h = hidden_cols(first, count)
            if first in SUMMED:
                b, turned = turned_sum[first]
                target, source = h.rearrange("p (j t) -> p j t", t=4), turned[:].rearrange("p t j -> p j t")
            else:
                b, turned = turned_pairs[first]
                target = h.rearrange("p (j u e) -> p j u e", u=2, e=2)
                source = turned[:].bitcast(BF16).rearrange("p u (j e) -> p j u e", e=2)
            if engine == "v":
                nc.vector.tensor_scalar_max(target, source, 0.0)
            else:
                nc.scalar.activation(target, source, RELU)

        def quantise_hidden(first, count=1):
            codes = keep.tile([P, P * count], U32, name="h_codes%d" % first, align_bytes=64)
            plane = keep.tile([P, P * count], U8, name="h_plane%d" % first, align_bytes=64)
            nc.vector.quantize_mx(out=codes[:].bitcast(FP8X4), scales=plane[:], in_=hidden_cols(first, count))
            for a in range(count):
                hidden_mx[first + a] = (codes[:, P * a : P * (a + 1)], plane[:, P * a : P * (a + 1)])
            hidden_mx[first, count] = (codes[:], plane[:])

        def second_layer(first, *banks):
            for jt, b in enumerate(banks, first):
                codes, plane = hidden_mx[jt]
                acc = bank(b, [P, 4, P])
                for t in range(4):
                    nc.tensor.matmul_mx(
                        out=acc[:, t, :],
                        lhsT=w2_codes[:, P * t : P * (t + 1)].bitcast(FP8X4),
                        lhsT_scale=w2_plane[:, P * t : P * (t + 1)],
                        rhs=codes.bitcast(FP8X4),
                        rhs_scale=plane,
                        start=True,
                        stop=True,
                    )
                products[jt] = (b, acc)

        def second_layer_wide(first, *banks):
            codes, plane = hidden_mx[first, 2]
            res, a = result[first]
            for half, b in enumerate(banks):
                acc = bank(b, [P, 2, 2 * P])
                for t in range(2 * half, 2 * half + 2):
                    nc.tensor.matmul_mx(
                        out=acc[:, t % 2, :],
                        lhsT=w2_codes[:, P * t : P * (t + 1)].bitcast(FP8X4),
                        lhsT_scale=w2_plane[:, P * t : P * (t + 1)],
                        rhs=codes.bitcast(FP8X4),
                        rhs_scale=plane,
                        start=True,
                        stop=True,
                    )
                products[first + half] = (b, acc)

        def empty_half(first, half):
            res, a = result[first]
            rows = slice(2 * half, 2 * half + 2)
            nc.scalar.copy(res[:, rows, :], products[first + half][1][:])
            nc.sync.dma_start(out_rows[:, rows, P * first : P * (first + 2)], res[:, rows, :])

        def empty(jt, engine="s"):
            b, acc = products[jt]
            res, a = result[jt]
            copier(engine)(res[:, :, P * a : P * (a + 1)], acc[:])

        def store(first):
            res, a = result[first]
            nc.sync.dma_start(out_rows[:, :, P * first : P * first + res[:].shape[2]], res[:])

        rounded = keep.tile([P, 4 * S], BF16, name="rounded", align_bytes=64)

        def rounded_cols(first, count):
            return rounded[:, 4 * P * first : 4 * P * (first + count)]

        def round_bank(jt, engine="s"):
            b, acc = products[jt]
            copier(engine)(
                rounded_cols(jt, 1).rearrange("p (j t) -> p j t", t=4),
                acc[:].rearrange("p t j -> p j t"),
            )

        def round_result(first, count=1, engine="v"):
            res, a = result[first]
            target = rounded_cols(first, count)
            source = res[:, :, P * a : P * (a + count)]
            if engine == "g":
                nc.gpsimd.tensor_scalar(
                    target.rearrange("p (j t) -> p j t", t=4),
                    source.rearrange("p t j -> p j t"),
                    1.0,
                    -0.0,
                    MULT,
                    ADD,
                )
            else:
                copier(engine)(
                    target.rearrange("p (c i t) -> p c t i", i=4, t=4), source.rearrange("p t (c i) -> p c t i", i=4)
                )

        def quantise_result(first, count=1):
            cols = slice(P * first, P * (first + count))
            nc.vector.quantize_mx(
                out=out_codes[:, cols].bitcast(FP8X4),
                scales=out_plane[4 * (first // 4) : P, P * (first % 4) : P * (first % 4 + count)],
                in_=rounded_cols(first, count),
            )

        def store_words(first, last):
            done = slice(P * first, P * last)
            nc.sync.dma_start(out_words[:, done], out_codes[:, done].bitcast(I32))

        for b, jt in enumerate(EARLY):
            product_pass(jt, 0, b)
        close(0)
        close(1)
        close(2)
        close(3)
        combine(0)
        combine(1)
        close(4)
        close(5)
        combine(2)
        combine(3)
        turn(0)
        rectify(0, 1, "s")
        turn(1)
        turn(2, 1, 0)
        turn(3, 1, 1)
        rectify(1, 1, "s")
        rectify(2, 1, "s")
        combine(4)
        close(6, 2)
        quantise_hidden(0)
        close(7, 4)
        second_layer(0, 3)
        rectify(3, 1)
        quantise_hidden(1)
        second_layer(1, 6)
        empty(0)
        store(0)
        combine(5)
        turn(4, 2, 7)
        quantise_hidden(2, 2)
        round_result(0, 1, "g")
        empty(1)
        store(1)
        second_layer(2, 5, 1)
        combine(6)
        combine(7)
        turn(6, 2, 0)
        empty(2)
        empty(3)
        store(2)
        rectify(4, 2)
        round_bank(1)
        round_bank(2)
        quantise_hidden(4, 2)
        second_layer_wide(4, 2, 3)
        rectify(6, 2)
        quantise_result(0, 2)
        store_words(0, 2)
        quantise_hidden(6, 2)
        second_layer(6, 4, 7)
        round_result(3)
        empty_half(4, 0)
        empty_half(4, 1)
        quantise_result(2, 2)
        store_words(2, 4)
        empty(6, "v")
        round_result(4, 2)
        empty(7)
        store(6)
        round_bank(7)
        round_result(6)
        quantise_result(4, 2)
        quantise_result(6)
        store_words(4, 7)
        quantise_result(7)
        store_words(7, 8)

        for q in range(4):
            nc.scalar.dma_start(
                out_2[0, 4 * q : 4 * q + 4, :].bitcast(I32).rearrange("r (c j) -> c r j", c=2),
                out_plane[32 * q : 32 * q + 8, :].bitcast(I32),
            )
